import numpy as np, ml_dtypes
CORES = [242,247,114,119]
N = 4
BF = ml_dtypes.bfloat16
S, L, RO, WEAR = 2176, 256, 3, 8
def near(rng, home, h):
    q = S // 16
    return np.take_along_axis(np.broadcast_to(home, (N, 8, S)), h * q + rng.integers(0, q, h.shape), 2)
def parts(rng):
    home = np.argsort(rng.random((8, S)), axis=1); hab = np.zeros((8, S), np.int64)
    np.put_along_axis(hab, home, np.broadcast_to(np.arange(S) // (S // 16), (8, S)), 1)
    base = rng.integers(0, 256, (N, 8, 16, 16))
    x = np.clip(np.take_along_axis(base, hab[None, :, None, :], 3) + rng.integers(-60, 61, (N, 8, 16, S)), 0, 255)
    lab = np.argsort(rng.random((N, 8, L)), axis=2); inv = np.argsort(lab, axis=2)
    h = np.broadcast_to((lab % 16)[:, :, None, :], (N, 8, 16, L)).reshape(N, 8, 16 * L)
    m = np.where(rng.random(h.shape) < 0.75, near(rng, home, h), rng.integers(0, S, h.shape)).reshape(N, 8, 16, L)
    h = np.broadcast_to(hab[None, :, None, :], (N, 8, 16, S)).reshape(N, 8, 16 * S)
    nb = np.where(rng.random(h.shape) < 0.6, near(rng, home, h), rng.integers(0, S, h.shape)).reshape(N, 8, 16, S)
    v = hab[None] + 16 * rng.integers(0, L // 16, (N, 8, S))
    own = np.where(rng.random((N, 8, S)) < 0.6, np.take_along_axis(inv, v, 2), rng.integers(0, L, (N, 8, S)))
    return x, nb, m, own, rng.integers(600, 1100, (N, 8))
def pack(x, nb, m, own, th):
    return {"x0": x.reshape(N, 128, S).astype(np.float32).astype(BF), "nb": nb.reshape(N, 128, S).astype(np.int32), "m0": m.reshape(N, 128, L).astype(np.int32),
            "own0": own.reshape(N, 8, S).astype(np.int32), "th": th.reshape(N, 8, 1).astype(np.int32)}
def setup_inputs(rng):
    return pack(*parts(rng))
def setup_inputs_ties(rng):
    x, nb, m, own, th = parts(rng); step = rng.choice(np.array([1, 5, 40]), (N, 8, 1, 1))
    lo = ((256 - 3 * step) * rng.random((N, 8, 1, 1)) * (rng.random((N, 8, 1, 1)) < 0.7)).astype(np.int64)
    x = lo + step * rng.integers(0, 4, x.shape)
    pool = rng.integers(0, S, (N, 8, 3, L)); few = np.take_along_axis(pool, rng.integers(0, 3, m.shape), 2)
    m = np.where(rng.random((N, 8, 1, L)) < 0.7, few, rng.integers(0, S, m.shape))
    th = step[:, :, 0, 0] * rng.integers(14, 19, (N, 8))
    z = int(rng.integers(0, 8)); o = rng.permutation(S); cold, warm = o[:S // 2], o[S // 2:]; h = rng.integers(140, 250, N)
    is_cold = np.zeros(S, bool); is_cold[cold] = True
    x[:, z] = np.where(is_cold, 0, h[:, None, None]) + rng.integers(0, 2, (N, 16, S))
    three = cold[rng.integers(0, S // 2, (N, 3, L))]; m[:, z] = np.take_along_axis(three, rng.integers(0, 3, (N, 16, L)), 1)
    nb[:, z] = warm[rng.integers(0, S - S // 2, (N, 16, S))]; th[:, z] = 16 * h + rng.integers(3, 9, N)
    return pack(x, nb, m, own, th)
def setup_inputs_corners(rng):
    x, nb, m, own, th = parts(rng); K = S // L; ev = (K + 1) // 2; od = K // 2
    q = int(rng.integers(0, N)); p = (q - 1) % N; u = (q - 2) % N; la = np.arange(L); st = np.arange(S)
    turn = [rng.permutation(8) for r in range(N)]; turn[u] = turn[p]
    for r in range(N):
        for i, g in enumerate(turn[r]):
            if i == 0: own[r, g] = int(rng.choice(np.array([0, L - 1, L // 2])))
            if i == 1:
                own[r, g] = rng.permutation(L)[st % L]; m[r, g] = la + L * rng.integers(0, K, (16, L))
            if i == 2: m[r, g] = rng.choice(np.array([0, S - 1, int(rng.integers(0, S))]), (1, L))
            if i == 3: nb[r, g] = st[None, :]
            if i == 4: nb[r, g] = (S - 1) * rng.integers(0, 2, (1, S))
            if i == 5:
                th[r, g] = 0; x[r, g] = rng.integers(0, WEAR + 2, (16, S))
            if i == 6:
                th[r, g] = 4080; own[r, g] = (L - 1) * rng.integers(0, 2, S); m[r, g] = (S - 1) * rng.integers(0, 2, (16, L))
            if i == 7: x[r, g] = int(rng.choice(np.array([0, 7, 255])))
    x[q] = np.where((st // L) % 2 == 0, rng.integers(0, 9, (8, 16, S)), 255 - rng.integers(0, 9, (8, 16, S)))
    x[q] = np.where(st // L == 1, rng.integers(18, 21, (8, 16, S)), x[q])
    nb[q] = rng.integers(0, L, (8, 16, S)) + 2 * L * rng.integers(0, ev, (8, 16, S)); th[q] = 200
    own[q] = np.argsort(rng.random((8, L)), axis=1)[:, st % L]
    m[q] = la + L * (2 * rng.integers(1, od, (8, 16, L)) + 1); m[p] = la + 2 * L * rng.integers(0, ev, (8, 16, L))
    m[u, int(turn[u][0])] = L + la
    return pack(x, nb, m, own, th)
def setup_inputs_ends(rng):
    home = 1 + np.argsort(rng.random((8, S - 3)), axis=1)[:, :L]; homes = np.broadcast_to(home, (N, 8, L))
    c = rng.choice(np.array([0, 1, 8, 15, 16]), (N, 8)); c[0, 0] = 0; c[0, 1] = 16; c[N - 1] = rng.choice(np.array([1, 8, 15]), 8)
    x = 255 * rng.integers(0, 2, (N, 8, 16, S))
    x[..., 0] = 255 * (np.argsort(rng.random((N, 8, 16)), axis=2) < c[:, :, None]); x[..., S - 1] = 255 - x[..., 0]; x[..., S - 2] = 255
    np.put_along_axis(x, np.broadcast_to(home[None, :, None, :], (N, 8, 16, L)), 0, 3)
    nb = (S - 1) * rng.integers(0, 2, (N, 8, 16, S))
    nb = np.where(rng.random(nb.shape) < 0.15, np.take_along_axis(homes, rng.integers(0, L, (N, 8, 16 * S)), 2).reshape(nb.shape), nb)
    side = rng.integers(0, 2, (N, 8, S)); nb[:, :, 15] = (S - 1) * side; nb[:, :, 0] = (S - 1) * (1 - side)
    sig = np.argsort(rng.random((N, 8, L)), axis=2); own = (L - 1) * rng.integers(0, 2, (N, 8, S)); np.put_along_axis(own, homes, sig, 2)
    mix = (S - 1) * rng.integers(0, 2, (N, 8, 16, L)); kind = rng.choice(np.array([0, 1, 2, 3, 3, 3]), (N, 8, 1, L)); kind[N - 2] = 3; kind[N - 1] = rng.integers(0, 2, (8, 1, L))
    place = np.argsort(rng.random((N, 8, 16, L)), axis=2); place[:, :, :, L - 1] = np.array([2, 3, 4, 5, 6, 7, 8, 9, 10, 11, 12, 13, 14, 15, 0, 1])
    two = rng.random((N, 8, 1, L)) < 0.5; two[..., L - 1] = True
    far = np.where((place == 1) | ((place == 2) & two), S - 2, mix)
    keep = np.where((place == 0) | ((place == 3) & two), home[None, :, None, :], far)
    m = np.where(kind == 0, 0, np.where(kind == 1, S - 1, np.where(kind == 2, mix, keep)))
    th = 4080 * rng.integers(0, 2, (N, 8)); th[:, 2] = 0; th[:, 7] = 4080
    i = int(rng.integers(0, 7)); th[N - 1] = 4080; th[N - 1, i] = 0
    g = (i + 1 + int(rng.integers(0, 6))) % 7; a = int(rng.integers(0, L)); nb[N - 1, g, :, home[g, a]] = m[N - 1, g, 0, sig[N - 1, g, a]]
    return pack(x, nb, m, own, th)
def setup_inputs_spread(rng):
    x, nb, m, own, th = parts(rng)
    x = np.minimum(np.exp2(8 * rng.random((N, 8, 1, S))) * rng.random((N, 8, 16, S)) * 1.25, 255.0).astype(np.int64) * (rng.random((N, 8, 1, S)) > 0.0625)
    m = np.minimum((S * rng.random((N, 8, 16, L)) ** (1 + 3 * rng.random((N, 8, 1, L)))).astype(np.int64), S - 1)
    m = np.where(rng.random((N, 8, 1, L)) < 0.5, m, S - 1 - m)
    u = np.minimum((S * rng.random((N, 4, 16, S)) ** 2).astype(np.int64), S - 1); nb[:, 1::2] = u
    own = np.minimum((L * rng.random((N, 8, S)) ** 2).astype(np.int64), L - 1)
    return pack(x, nb, m, own, np.exp2(8 + 3 * rng.random((N, 8))).astype(np.int64))
def check_inputs(d):
    bad = []
    for k, lo, hi in (("x0", 0, 255), ("nb", 0, S - 1), ("m0", 0, S - 1), ("own0", 0, L - 1), ("th", 0, 4080)):
        try:
            v = np.asarray(d[k]).astype(np.float32).astype(np.float64)
            if not np.all((v >= lo) & (v <= hi)): bad.append("range of " + k)
            elif not np.all(v == np.floor(v)): bad.append("whole numbers of " + k)
        except Exception:
            bad.append("form of " + k)
    return bad
def centre(x, m):
    v = np.take_along_axis(x, m.reshape(8, 1, 16 * L), 2).reshape(8, 16, 16, L)
    c = (np.max(v, axis=2) + np.min(v, axis=2)) >> 1
    d = np.add.reduce(np.abs(v - c[:, :, None, :]), axis=1)
    return c, np.argmin(d, axis=1), np.argmax(d, axis=1)
def reference(x0, nb, m0, own0, th):
    X = x0.astype(np.float32).astype(np.int32).reshape(N, 8, 16, S); nbs = nb.astype(np.int64).reshape(N, 8, 16, S)
    M = m0.astype(np.int64).reshape(N, 8, 16, L); O = own0.astype(np.int64).reshape(N, 8, S); T = th.astype(np.int64).reshape(N, 8)
    wins = np.zeros(N, np.int64); lane = np.broadcast_to(np.arange(L), (8, L)); grp = np.broadcast_to(np.arange(8)[:, None], (8, L))
    for t in range(RO):
        res, back = [], []; now = np.zeros(N, np.int64)
        for q in range(N):
            p = (q - 1 - t % (N - 1)) % N
            ci, ki, fi = centre(X[q], M[p]); cr, kr, fr = centre(X[q], M[q])
            s = np.take_along_axis(M[p], ki[:, None, :], 1)[:, 0]
            b = np.take_along_axis(O[q], s, 1)
            low = np.full((8, L), L); np.minimum.at(low, (grp, b), lane)
            fight = np.take_along_axis(low, b, 1) == lane
            n = np.take_along_axis(nbs[q], s[:, None, :], 2)
            v = np.take_along_axis(X[q], n.reshape(8, 1, 16 * L), 2).reshape(8, 16, 16, L)
            ei = np.add.reduce(np.abs(v - ci[:, :, None, :]), axis=1)
            er = np.add.reduce(np.abs(v - np.take_along_axis(cr, b[:, None, :], 2)[:, :, None, :]), axis=1)
            lim = T[q][:, None, None] + (wins[q] & 63)
            won = np.count_nonzero(ei < lim, axis=1) > np.count_nonzero(er < lim, axis=1)
            e = np.where(won[:, None, :], ei, er)
            best = np.take_along_axis(n, np.argmin(e, axis=1)[:, None, :], 1)[:, 0]
            worst = np.take_along_axis(n, np.argmax(e, axis=1)[:, None, :], 1)[:, 0]
            g, a = np.nonzero(fight); w = won[g, a]; bb = b[g, a]; ss = s[g, a]
            res.append((q, g, fr[g, bb], bb, np.where(w, worst[g, a], best[g, a])))
            back.append((p, g, np.where(w, fi[g, a], ki[g, a]), a, np.where(w, best[g, a], worst[g, a])))
            O[q][g, ss] = np.where(w, np.where(bb + 1 == L, 0, bb + 1), bb)
            if t < RO - 1: X[q][g, :, ss] = np.maximum(X[q][g, :, ss] - WEAR, 0)
            now[q] = np.count_nonzero(w)
        for r, g, k, a, z in res + back: M[r][g, k, a] = z
        wins = now
    return {"ym": M.reshape(N, 128, L).astype(np.float32), "yown": O.astype(np.float32)}

@@ -1,0 +1,512 @@
+from concourse.mybir import dt, AluOpType, AxisListType, ActivationFunctionType
+
+S, L, RO = 2176, 256, 3
+SW = 2560
+ZW = 640
+OP = AluOpType
+AF = ActivationFunctionType
+
+SCRATCH = {}
+ALIAS = {}
+
+
+def _d(name, where, shape, dtype):
+    SCRATCH[name] = (where, shape, dtype)
+
+
+for _n, _c, _t in [
+        ("Xw", SW, "bfloat16"), ("OWw", SW, "bfloat16"), ("NBw", S, "int32"), ("ZRw", ZW, "float32"),
+        ("Mi", 256, "int32"), ("Tm", 256, "int32"), ("Tm2", 256, "int32"), ("Mo", 256, "float32"),
+        ("oi", 136, "int32"), ("ob", 136, "bfloat16"),
+        ("vR", 4096, "bfloat16"), ("vI", 4096, "bfloat16"), ("vN", 4096, "bfloat16"),
+        ("mxA", 2048, "bfloat16"), ("mnA", 2048, "bfloat16"), ("mxB", 2048, "bfloat16"), ("mnB", 2048, "bfloat16"),
+        ("tt", 256, "float32"), ("ti", 256, "int32"),
+        ("CR", 256, "bfloat16"), ("CI", 256, "bfloat16"), ("CB", 256, "bfloat16"),
+        ("TR", 256, "bfloat16"), ("TI", 256, "bfloat16"), ("TB", 256, "bfloat16"),
+        ("mA", 2048, "bfloat16"), ("mB", 2048, "bfloat16"), ("mC", 2048, "bfloat16"),
+        ("Fs", 512, "float32"), ("nw", 512, "float32"), ("np", 512, "float32"),
+        ("RSR", 256, "float32"), ("RSI", 512, "float32"), ("NSI", 512, "float32"), ("NSR", 512, "float32"),
+        ("MF", 256, "float32"), ("SRs", 256, "float32"), ("SIs", 256, "float32"),
+        ("rm", 256, "bfloat16"), ("RM", 256, "bfloat16"), ("ex", 256, "float32"),
+        ("nU", 256, "uint16"), ("nF", 256, "float32"), ("bG", 256, "bfloat16"), ("dm", 256, "bfloat16"),
+        ("bs", 256, "bfloat16"), ("EQ", 4096, "bfloat16"), ("fG", 256, "bfloat16"),
+        ("fd", 256, "bfloat16"), ("fs", 256, "bfloat16"), ("vS", 256, "bfloat16"), ("vT", 256, "bfloat16"),
+        ("fI", 256, "bfloat16"), ("fR", 256, "bfloat16"), ("PC", 272, "float32"),
+        ("mk2", 256, "float32"), ("DL", 256, "float32"), ("ez", 256, "float32"), ("zG", 256, "float32"),
+        ("wG", 256, "bfloat16"), ("ov", 256, "float32"), ("oq", 256, "float32"), ("ow", 256, "float32"),
+        ("wf", 256, "float32"), ("Dr", 256, "float32"), ("TH", 128, "float32"), ("TH0", 128, "float32"),
+        ("sF32", 256, "float32"), ("sI32", 64, "int32"), ("sU16", 64, "uint16"), ("pi", 4, "int32"), ("pf", 8, "float32"),
+        ("E", 2048, "bfloat16"), ("one", 2048, "bfloat16"), ("m0", 1024, "bfloat16"), ("a0", 1024, "bfloat16"),
+        ("AK", 256, "float32"), ("mkf", 256, "float32"), ("BK", 256, "bfloat16"), ("BK1", 256, "bfloat16"),
+        ("BC", 256, "bfloat16"), ("BM", 16, "bfloat16"), ("BV", 16, "bfloat16"), ("KR", 256, "bfloat16"),
+        ("Ib", 128, "bfloat16"), ("If", 128, "float32"), ("W1", 128, "bfloat16"), ("W2", 128, "bfloat16"),
+        ("W0", 128, "bfloat16"), ("thr", 256, "float32"), ("pw", 256, "float32"), ("pv", 256, "float32"),
+        ("CC", 8, "float32"), ("MI", 256, "float32"), ("MIb", 256, "bfloat16"), ("ii", 256, "float32"),
+        ("bi", 16, "int32"), ("ks", 32, "float32"), ("o6", 128, "float32"), ("B8", 128, "float32")]:
+    _d("c_" + _n, "sbuf", [128, _c], _t)
+for _k, _n in enumerate(("lR", "sF", "w1", "w2", "dc", "won", "d1", "d2", "d3", "zi", "zr", "ch")):
+    ALIAS[_n] = ("c_sF32", 16 * _k, 16)
+for _k, _n in enumerate(("wc", "w16", "thf")):
+    ALIAS[_n] = ("c_sF32", 192 + 16 * _k, 1)
+for _k, (_n, _c) in enumerate((("pk", 16), ("si", 16), ("wi", 1), ("wj", 1))):
+    ALIAS[_n] = ("c_sI32", 16 * _k, _c)
+_d("c_thi", "sbuf", [128, 1], "int32")
+for _k, _n in enumerate(("sU", "bU", "sWU", "bWU")):
+    ALIAS[_n] = ("c_sU16", 16 * _k, 16)
+_d("c_BL", "sbuf", [128, 16], "uint16")
+for _t in range(RO):
+    _d("Mu%d" % _t, "sbuf", [128, 256], "uint16")
+    _d("Lin%d" % _t, "sbuf", [128, 256], "uint16")
+    _d("Do%d" % _t, "sbuf", [128, 256], "float32")
+    _d("Din%d" % _t, "sbuf", [128, 256], "float32")
+for _n in ("BC0", "BC1", "BC2", "KE0", "KE1", "SIT", "MS0", "MS1"):
+    _d("p_" + _n, "psum", [128, 512], "float32")
+_d("ownd", "dram", [8, S], "bfloat16")
+
+SEMAPHORES = (["qV", "qS", "qP", "qG", "dx", "dm", "dn", "do", "dod", "dor", "dth", "dy", "dyo"]
+              + ["aL%d" % t for t in range(RO)] + ["aD%d" % t for t in range(RO)]
+              + ["lL%d" % t for t in range(RO)] + ["lD%d" % t for t in range(RO)])
+
+
+def rank_program(g, core, T, topo):
+    rank = T.rank_of(core)
+    if rank is None:
+        return
+    N = len(T.cores)
+    Q = {"V": g.vector, "S": g.scalar, "P": g.tensor, "G": g, "Y": g.sync}
+    cnt = {"V": 0, "S": 0, "P": 0, "G": 0}
+    known = {q: {} for q in Q}
+    snap = {}
+    acc = {}
+    total = {}
+
+    def R(name, c0=0, c1=None, st=1, p0=0, p1=128):
+        o = 0
+        if name in ALIAS:
+            name, o, w = ALIAS[name]
+        else:
+            if not (name in SCRATCH):
+                name = "c_" + name if "c_" + name in SCRATCH else "p_" + name
+            w = SCRATCH[name][1][1]
+        c1 = o + (w if c1 is None else c1)
+        c0 = o + c0
+        ap = T[name][p0:p1, c0:c1] if st == 1 else T[name][p0:p1, c0:c1:st]
+        return (ap, name, c0, c1)
+
+    def ind(win, off):
+        return win[0].indirect(off[0])
+
+    def need(queue, reads, writes):
+        out = {}
+        for regs, wr in ((reads, False), (writes, True)):
+            for r in regs:
+                ps = r[1].startswith("p_")
+                for (c0, c1, q, src, n, w) in acc.get(r[1], []):
+                    if ps:
+                        if q == queue == "P":
+                            continue
+                        if q == queue and (not w or wr or c0 >= r[3] or r[2] >= c1):
+                            continue
+                    else:
+                        if c0 >= r[3] or r[2] >= c1 or not (w or wr):
+                            continue
+                        if q == queue and q in cnt and not w:
+                            continue
+                    out[src] = max(out.get(src, 0), n)
+        return out
+
+    def learn(queue, src, n):
+        k = known[queue]
+        k[src] = max(k.get(src, 0), n)
+        for s2, n2 in snap.get((src, n), {}).items():
+            k[s2] = max(k.get(s2, 0), n2)
+
+    def waits(queue, nd):
+        for src in sorted(nd, key=lambda s: -nd[s]):
+            if known[queue].get(src, 0) < nd[src]:
+                Q[queue].wait_ge(T.sem[src], nd[src])
+                learn(queue, src, nd[src])
+
+    def note(queue, src, n, reads, writes):
+        snap[(src, n)] = dict(known[queue])
+        for regs, wr in ((reads, False), (writes, True)):
+            for r in regs:
+                lst = acc.get(r[1], [])
+                if wr:
+                    lst = [e for e in lst if not (e[0] >= r[2] and e[1] <= r[3])]
+                acc[r[1]] = lst + [(r[2], r[3], queue, src, n, wr)]
+
+    def op(queue, fn, reads, writes):
+        waits(queue, need(queue, reads, writes))
+        inst = fn()
+        cnt[queue] += 1
+        inst.then_inc(T.sem["q" + queue], 1)
+        total["q" + queue] = cnt[queue]
+        note(queue, "q" + queue, cnt[queue], reads, writes)
+
+    def act(out, in_, off=None):
+        src = in_[0] if off is None else ind(in_, off)
+        op("S", lambda: g.scalar.activation(out[0], src, AF.Copy), [in_] + ([off] if off else []), [out])
+
+    def cp(out, in_, off=None):
+        src = in_[0] if off is None else ind(in_, off)
+        op("V", lambda: g.vector.tensor_copy(out[0], src), [in_] + ([off] if off else []), [out])
+
+    def scat(win, off, in_):
+        op("V", lambda: g.vector.tensor_copy(ind(win, off), in_[0]), [in_, off], [win])
+
+    def tt(out, a, b, o, off=None):
+        src = a[0] if off is None else ind(a, off)
+        op("V", lambda: g.vector.tensor_tensor(out[0], src, b[0], o), [a, b] + ([off] if off else []), [out])
+
+    def ts(out, a, s1, o1, s2=None, o2=None):
+        rd = [a]
+        x1 = s1
+        if isinstance(s1, tuple):
+            rd.append(s1)
+            x1 = s1[0]
+        if o2 is None:
+            op("V", lambda: g.vector.tensor_scalar(out[0], a[0], x1, None, o1), rd, [out])
+        else:
+            op("V", lambda: g.vector.tensor_scalar(out[0], a[0], x1, s2, o1, o2), rd, [out])
+
+    def scan(out, a, b, o1, o2, init=0.0):
+        op("V", lambda: g.vector.tensor_tensor_scan(out[0], a[0], b[0], init, o1, o2), [a, b], [out])
+
+    def fill(out, x):
+        op("V", lambda: g.vector.memset(out[0], x), [], [out])
+
+    def mm(out, l, r, start=True, stop=True):
+        op("P", lambda: g.tensor.matmul(out[0], l[0], r[0], start, stop), [l, r], [out])
+
+    def rsum(out, in_):
+        op("V", lambda: g.vector.tensor_reduce(out[0], in_[0], AxisListType.X, OP.add), [in_], [out])
+
+    def iota(out, pat, base, mult):
+        op("G", lambda: g.iota(out[0], pat, base, mult, allow_small_or_imprecise_dtypes=True), [], [out])
+
+    def asel(out, in_, pat, cmp_, base, mult):
+        op("G", lambda: g.affine_select(out[0], in_[0], pat, cmp_, 0.0, base, mult), [in_], [out])
+
+    def dma(sem, pairs, reads, writes):
+        waits("Y", need("Y", reads, writes))
+        for o, i in pairs:
+            g.sync.dma_start(o, i).then_inc(T.sem[sem], 16)
+        total[sem] = 16 * len(pairs)
+        note("Y", sem, total[sem], reads, writes)
+
+    def send(buf, land, dst, asem, lsem):
+        eng = topo.engines(core, dst)[:8]
+        m = 0
+        for e in eng:
+            m |= 1 << e
+        waits("G", need("G", [buf], []))
+        rid, pid = topo.addr(dst, core)
+        g.remote_dma(T[land][:], buf[0], T.sem[asem], T.sem[lsem], pid, rid, m)
+        total[lsem] = len(eng)
+
+    def arrive(land, asem, src):
+        n = len(topo.engines(src, core)[:8])
+        total[asem] = n
+        acc[land] = [(0, 256, "X", asem, n, True)]
+
+    dma("dm", [(T.c_Mi[:, :], T.m0[:, :])], [], [R("Mi")])
+    dma("dx", [(T.c_Xw[:, 0:S], T.x0[:, :])], [], [R("Xw", 0, S)])
+    dma("do", [(T.c_oi[:, :], T.own0[:, :])], [], [R("oi")])
+    dma("dth", [(T.c_thi[0:8, :], T.th[:, :])], [], [R("thi", 0, 1)])
+    dma("dn", [(T.c_NBw[:, :], T.nb[:, :])], [], [R("NBw")])
+    fill(R("m0"), 1.0)
+    fill(R("a0"), 0.0)
+    fill(R("one"), 1.0)
+    fill(R("m0", 0, 1024, 16), 0.0)
+    fill(R("a0", 0, 1024, 16), 512.0)
+    cp(R("Mu0"), R("Mi"))
+    for t in range(RO):
+        arrive("Lin%d" % t, "aL%d" % t, T.cores[(rank - 1 - t) % N])
+        arrive("Din%d" % t, "aD%d" % t, T.cores[(rank + 1 + t) % N])
+    iota(R("pi", 0, 1), [[0, 1]], 0, 1)
+    iota(R("bi"), [[1, 16]], 0, 0)
+    asel(R("Ib"), R("one", 0, 128), [[-1, 128]], OP.is_equal, 0, 1)
+    send(R("Mu0"), "Lin0", T.cores[(rank + 1) % N], "aL0", "lL0")
+    asel(R("E"), R("one"), [[-1, 128], [0, 16]], OP.is_equal, 0, 1)
+    asel(R("BK1"), R("one", 0, 256), [[0, 2], [-16, 8], [0, 16]], OP.is_ge, 0, 1)
+    asel(R("BK"), R("BK1"), [[0, 2], [16, 8], [0, 16]], OP.is_ge, 15, -1)
+    iota(R("KR"), [[-15, 2], [0, 8], [1, 16]], 0, 0)
+    iota(R("ii"), [[0, 16], [1, 16]], 0, 0)
+    iota(R("ks", 0, 16), [[16, 16]], S, 1)
+    iota(R("ks", 16, 32), [[16, 16]], 256, 1)
+
+    def consts_early():
+        cp(R("ob"), R("oi"))
+        dma("dod", [(T.ownd[:, :], T.c_ob[:, :])], [R("ob")], [("", "ownd", 0, S)])
+        dma("dor", [(T.c_OWw[i::16, 0:S], T.ownd[:, :]) for i in range(16)], [("", "ownd", 0, S)], [R("OWw", 0, S)])
+        ts(R("pi", 1, 2), R("pi", 0, 1), 15, OP.bitwise_and)
+        cp(R("pf", 0, 1), R("pi", 1, 2))
+        ts(R("pf", 1, 2), R("pf", 0, 1), 1.0, OP.add, 4096.0, OP.mult)
+        ts(R("MF"), R("Mu0"), R("pf", 1, 2), OP.add)
+        cp(R("If"), R("Ib"))
+        cp(R("BL"), R("bi"))
+
+    def consts_mid():
+        ts(R("BM", 0, 8), R("BK", 0, 128, 16), 32.0, OP.mult)
+        ts(R("BM", 8, 16), R("BK", 0, 128, 16), -32.0, OP.mult)
+        ts(R("BV", 0, 8), R("BK", 0, 128, 16), -16.0, OP.mult)
+        ts(R("BV", 8, 16), R("BK", 0, 128, 16), 16.0, OP.mult)
+        ts(R("BC", 0, 128), R("BK", 0, 128), -16.0, OP.mult)
+        ts(R("BC", 128, 256), R("BK", 0, 128), 16.0, OP.mult)
+        fill(R("AK"), 0.0)
+        fill(R("mkf"), 1.0)
+        fill(R("AK", 0, 256, 16), 1000000.0)
+        fill(R("mkf", 0, 256, 16), 0.0)
+        ts(R("MI"), R("ii"), R("pf", 0, 1), OP.is_equal)
+        cp(R("MIb"), R("MI"))
+        cp(R("CC"), R("BK", 0, 128, 16))
+
+    def consts_late():
+        fill(R("pw"), 0.0)
+        fill(R("pw", 0, 256, 16), 2.0)
+        ts(R("pv"), R("mkf"), 0.5, OP.mult)
+        scan(R("thr"), R("pv"), R("pw"), OP.mult, OP.add)
+        tt(R("wf", 0, 16), R("thr", 0, 16), R("MI", 0, 16), OP.mult)
+        rsum(R("pf", 2, 3), R("wf", 0, 16))
+        ts(R("W1"), R("BK", 0, 128), 64.0, OP.mult)
+        ts(R("W2"), R("BK", 0, 128), R("pf", 2, 3), OP.mult, 0.5, OP.mult)
+        fill(R("W0"), 0.0)
+        fill(R("o6"), 0.0625)
+        fill(R("PC", 0, 16), 0.0)
+        cp(R("thf", 0, 1, 1, 0, 8), R("thi", 0, 1, 1, 0, 8))
+        ts(R("B8", 0, 128, 1, 0, 8), R("E", 0, 128, 1, 0, 8), R("thf", 0, 1, 1, 0, 8), OP.mult, 256.0, OP.mult)
+        mm(R("MS1", 0, 128), R("o6", 0, 128, 1, 0, 8), R("B8", 0, 128, 1, 0, 8))
+        cp(R("TH0"), R("MS1", 0, 128))
+
+    def gather(v, lst, h):
+        for c in range(2):
+            a = h * 128 + c * 64
+            act(R(v, a * 16, a * 16 + 1024), R("Xw", 0, S), R(lst, a, a + 64))
+
+    def scans(v, h, C, bufs):
+        mx, mn = bufs
+        for c in range(2):
+            x = R(v, h * 2048 + c * 1024, h * 2048 + c * 1024 + 1024)
+            scan(R(mx, c * 1024, c * 1024 + 1024), R("m0"), x, OP.mult, OP.max)
+            scan(R(mn, c * 1024, c * 1024 + 1024), R("a0"), x, OP.add, OP.min)
+        a, b = h * 128, h * 128 + 128
+        tt(R("tt", a, b), R(mx, 15, 2048, 16), R(mn, 15, 2048, 16), OP.add)
+        ts(R("ti", a, b), R("tt", a, b), 0.5, OP.mult, -0.25, OP.add)
+        cp(R(C, a, b), R("ti", a, b))
+
+    def turn(C, h):
+        mm(R("MS0", h * 128, h * 128 + 128), R(C, h * 128, h * 128 + 128), R("Ib"))
+
+    def turned(TC, h):
+        cp(R(TC, h * 128, h * 128 + 128), R("MS0", h * 128, h * 128 + 128))
+
+    bcn, ken, mbn, bank = [0], [0], [0], {}
+
+    def bc(u, b):
+        k = "BC%d" % (bcn[0] % 3)
+        bcn[0] += 1
+        bank[(u, b)] = k
+        mm(R(k), R(u[2], u[4] * 128, u[4] * 128 + 128), R("E", b * 512, b * 512 + 512))
+
+    def run_units(units, after):
+        flat = [(u, b) for u in units for b in range(4)]
+        for u, b in flat[:3]:
+            bc(u, b)
+        for n, (u, b) in enumerate(flat):
+            if b == 0:
+                mb = "m" + "ABC"[mbn[0] % 3]
+                mbn[0] += 1
+            x = R(u[1], u[4] * 2048 + b * 512, u[4] * 2048 + b * 512 + 512)
+            tt(R(mb, b * 512, b * 512 + 512), x, R(bank[(u, b)]), OP.max)
+            if n + 3 < len(flat):
+                bc(*flat[n + 3])
+            if b == 3:
+                ke = "KE%d" % (ken[0] % 2)
+                ken[0] += 1
+                h = u[4]
+                mm(R(ke, 0, 256), R("one", 0, 128, 1, 0, 1), R("KR", 0, 256, 1, 0, 1), True, False)
+                mm(R(ke, 0, 256), R(u[3], h * 128, h * 128 + 128), R("BC"), False, False)
+                for k in range(16):
+                    mm(R(ke, k, 256, 16), R(u[1], h * 2048 + k, h * 2048 + 2048, 16), R("BV"), False, False)
+                for k in range(16):
+                    mm(R(ke, k, 256, 16), R(mb, k, 2048, 16), R("BM"), False, k == 15)
+                after(u, ke)
+
+    def pick(ke, res, h, sit, xs, wide):
+        for x in xs:
+            k = R(ke, x * 128, x * 128 + 128)
+            o = x * 128
+            scan(R("Fs", o, o + 128), R("AK", 0, 128), k, OP.add, OP.min)
+            tt(R("nw", o, o + 128), k, R("Fs", o, o + 128), OP.is_equal)
+            tt(R("np", o, o + 128), R("nw", o, o + 128), R(sit, h * 128, h * 128 + 128), OP.mult)
+            d = (x * 256 if wide else 0) + h * 128
+            scan(R(res, d, d + 128), R("mkf", 0, 128), R("np", o, o + 128), OP.mult, OP.max)
+
+    def flip(src, ps, idn):
+        for h in range(2):
+            mm(R(ps, h * 128, h * 128 + 128), R(src, h * 128, h * 128 + 128), R(idn))
+
+    for t in range(RO):
+        last = t == RO - 1
+        mu, li, do = "Mu%d" % t, "Lin%d" % t, "Do%d" % t
+        kes = {}
+
+        def after(u, ke):
+            kes[(u[0], u[4])] = ke
+
+        gather("vR", mu, 0)
+        gather("vR", mu, 1)
+        if t == 0:
+            consts_early()
+        else:
+            ts(R("MF"), R(mu), R("pf", 1, 2), OP.add)
+        scans("vR", 0, "CR", ("mxA", "mnA"))
+        turn("CR", 0)
+        flip("MF", "SIT", "If")
+        if t == 0:
+            consts_mid()
+        scans("vR", 1, "CR", ("mxB", "mnB"))
+        turned("TR", 0)
+        turn("CR", 1)
+        gather("vI", li, 0)
+        gather("vI", li, 1)
+        act(R("SRs"), R("SIT", 0, 256))
+        turned("TR", 1)
+        run_units([("R", "vR", "TR", "CR", 0), ("R", "vR", "TR", "CR", 1)], after)
+        ts(R("MF"), R(li), R("pf", 1, 2), OP.add)
+        flip("MF", "MS1", "If")
+        scans("vI", 0, "CI", ("mxA", "mnA"))
+        pick(kes[("R", 0)], "RSR", 0, "SIT", [1], False)
+        turn("CI", 0)
+        pick(kes[("R", 1)], "RSR", 1, "SIT", [1], False)
+        scans("vI", 1, "CI", ("mxB", "mnB"))
+        turned("TI", 0)
+        turn("CI", 1)
+        act(R("SIs"), R("MS1", 0, 256))
+        cp(R("lR"), R("RSR", 15, 256, 16))
+        turned("TI", 1)
+        run_units([("I", "vI", "TI", "CI", 0), ("I", "vI", "TI", "CI", 1)], after)
+        tt(R("rm"), R("lR"), R("SRs"), OP.is_equal, R("BL"))
+        pick(kes[("I", 0)], "RSI", 0, "MS1", [0], True)
+        pick(kes[("I", 1)], "RSI", 1, "MS1", [0], True)
+        cp(R("pk"), R("RSI", 15, 256, 16))
+        ts(R("si"), R("pk"), 4095, OP.bitwise_and)
+        tt(R("ex"), R("si"), R("MI"), OP.mult, R("BL"))
+        for h in range(2):
+            mm(R("MS0", h * 8, h * 8 + 8), R("ex", h * 128, h * 128 + 128), R("CC"))
+        cp(R("sU"), R("MS0", 0, 16))
+        cp(R("nU"), R("NBw"), R("sU"))
+        for c in range(4):
+            act(R("vN", c * 1024, c * 1024 + 1024), R("Xw", 0, S), R("nU", c * 64, c * 64 + 64))
+        cp(R("sF"), R("sU"))
+        cp(R("bG"), R("OWw", 0, S), R("sU"))
+        tt(R("dm"), R("bG"), R("MIb"), OP.mult)
+        scan(R("bs"), R("m0", 0, 256), R("dm"), OP.mult, OP.add)
+        cp(R("bU"), R("bs", 15, 256, 16))
+        cp(R("CB"), R("CR"), R("bU"))
+        for h in range(2):
+            turn("CB", h)
+        for h in range(2):
+            pick(kes[("I", h)], "RSI", h, "MS1", [1], True)
+        for h in range(2):
+            turned("TB", h)
+        ts(R("nF"), R("nU"), R("pf", 1, 2), OP.add)
+        flip("nF", "SIT", "If")
+        if t == 0:
+            consts_late()
+            th = "TH0"
+        else:
+            mm(R("MS0", 0, 1), R("o6"), R("wc"))
+            cp(R("wi"), R("MS0", 0, 1))
+            ts(R("wj"), R("wi"), 63, OP.bitwise_and)
+            ts(R("w16"), R("wj"), 16.0, OP.mult)
+            ts(R("TH"), R("TH0"), R("w16"), OP.add)
+            th = "TH"
+
+        def judge(who, h):
+            ke, intr = kes[(who, h)], who == "NI"
+            pick(ke, "NSI" if intr else "NSR", h, "SIT", [0, 1], True)
+            tt(R("fI" if intr else "fR", h * 128, h * 128 + 128), R(ke, 0, 128), R(th), OP.is_lt)
+
+        run_units([("NI", "vN", "TI", "CI", 0), ("NR", "vN", "TB", "CB", 0)], after)
+        offs = [sum(256 - 16 * x for x in range(c)) for c in range(16)]
+        for c in range(16):
+            ts(R("EQ", offs[c], offs[c] + 256 - 16 * c), R("bG", 16 * c, 256), R("bs", 16 * c + 15, 16 * c + 16), OP.is_equal)
+        mm(R("MS1", 0, 256), R("W0"), R("EQ", 0, 256), True, False)
+        for c in range(16):
+            if c < 15:
+                mm(R("MS1", 16 * c + 16, 256), R("W1"), R("EQ", offs[c] + 16, offs[c] + 256 - 16 * c), False, False)
+            mm(R("MS1", 16 * c, 16 * c + 16), R("W2"), R("EQ", offs[c], offs[c] + 16), False, c == 15)
+        judge("NI", 0)
+        judge("NR", 0)
+        tt(R("fG"), R("MS1", 0, 256), R("thr"), OP.is_lt)
+        run_units([("NI", "vN", "TI", "CI", 1), ("NR", "vN", "TB", "CB", 1)], after)
+        flip("rm", "MS0", "Ib")
+        act(R("RM"), R("MS0", 0, 256))
+        tt(R("fd"), R("fG"), R("MIb"), OP.mult)
+        scan(R("fs"), R("m0", 0, 256), R("fd"), OP.mult, OP.add)
+        tt(R("w1"), R("sF"), R("ks", 0, 16), OP.subtract)
+        tt(R("w2"), R("bs", 15, 256, 16), R("ks", 16, 32), OP.subtract)
+        tt(R("w1"), R("w1"), R("fs", 15, 256, 16), OP.mult)
+        tt(R("w2"), R("w2"), R("fs", 15, 256, 16), OP.mult)
+        tt(R("w1"), R("w1"), R("ks", 0, 16), OP.add)
+        tt(R("w2"), R("w2"), R("ks", 16, 32), OP.add)
+        cp(R("sWU"), R("w1"))
+        cp(R("bWU"), R("w2"))
+        judge("NI", 1)
+        if not last:
+            cp(R("vS"), R("Xw", 0, S), R("sU"))
+            ts(R("vT"), R("vS"), -8.0, OP.add, 0.0, OP.max)
+        tt(R("d3"), R("RSI", 271, 512, 16), R("RSI", 15, 256, 16), OP.subtract)
+        judge("NR", 1)
+        scan(R("PC", 16, 272), R("fI"), R("fR"), OP.add, OP.subtract)
+        tt(R("dc"), R("PC", 31, 272, 16), R("PC", 15, 256, 16), OP.subtract)
+        ts(R("won"), R("dc"), 0.0, OP.is_gt)
+        tt(R("d1"), R("NSI", 15, 256, 16), R("NSR", 271, 512, 16), OP.subtract)
+        tt(R("d1"), R("d1"), R("won"), OP.mult)
+        tt(R("zi"), R("d1"), R("NSR", 271, 512, 16), OP.add)
+        tt(R("d3"), R("d3"), R("won"), OP.mult)
+        tt(R("ch"), R("d3"), R("RSI", 15, 256, 16), OP.add)
+        tt(R("mk2"), R("ch"), R("SIs"), OP.is_equal, R("BL"))
+        tt(R("DL"), R("zi"), R("mk2"), OP.mult, R("BL"))
+        flip("DL", "MS0", "If")
+        tt(R("d2"), R("NSI", 271, 512, 16), R("NSR", 15, 256, 16), OP.subtract)
+        ts(R("d2"), R("d2"), 262144.0, OP.add)
+        tt(R("d2"), R("d2"), R("won"), OP.mult)
+        tt(R("zr"), R("d2"), R("NSR", 15, 256, 16), OP.add)
+        act(R("ez"), R("zr"), R("BL"))
+        flip("ez", "MS1", "If")
+        tt(R(do), R("MS0", 0, 256), R("fG"), OP.mult)
+        send(R(do), "Din%d" % t, T.cores[(rank - 1 - t) % N], "aD%d" % t, "lD%d" % t)
+        act(R("zG"), R("MS1", 0, 256))
+        fill(R("ZRw", 0, 256), 0.0)
+        if not last:
+            scat(R("Xw"), R("sWU"), R("vT"))
+        scat(R("ZRw"), R("bWU"), R("zG"))
+        tt(R("Dr"), R("ZRw", 0, 256), R("RM"), OP.mult)
+        tt(R("Tm"), R("Mi"), R("Dr"), OP.max)
+        ts(R("wG"), R("zG"), 262144.0, OP.is_ge)
+        tt(R("ov"), R("bG"), R("wG"), OP.add)
+        ts(R("oq"), R("ov"), 256.0, OP.is_ge, -256.0, OP.mult)
+        tt(R("ow"), R("ov"), R("oq"), OP.add)
+        scat(R("OWw"), R("sWU"), R("ow"))
+        if last:
+            waits("G", need("G", [R("OWw", 0, S)], []))
+            g.dma_start(T.yown[:, :], T.c_OWw[0::16, 0:S]).then_inc(T.sem.dyo, 16)
+            total["dyo"] = 16
+        else:
+            tt(R("wf"), R("wG"), R("fG"), OP.mult)
+            rsum(R("wc"), R("wf"))
+        ts(R("Tm2"), R("Tm"), 4095, OP.bitwise_and)
+        tt(R("Tm"), R("Tm2"), R("Din%d" % t), OP.max)
+        ts(R("Mi"), R("Tm"), 4095, OP.bitwise_and)
+        if not last:
+            cp(R("Mu%d" % (t + 1)), R("Mi"))
+            send(R("Mu%d" % (t + 1)), "Lin%d" % (t + 1), T.cores[(rank + 2 + t) % N], "aL%d" % (t + 1), "lL%d" % (t + 1))
+        else:
+            cp(R("Mo"), R("Mi"))
+            dma("dy", [(T.ym[:, :], T.c_Mo[:, :])], [R("Mo")], [])
+    for s in sorted(total):
+        if known["G"].get(s, 0) < total[s]:
+            g.wait_ge(T.sem[s], total[s])

@@ -14,58 +14,37 @@ def _d(name, where, shape, dtype):
     SCRATCH[name] = (where, shape, dtype)
 
 
-for _n, _c, _t in [
-        ("Xw", SW, "bfloat16"), ("OWw", SW, "bfloat16"), ("NBw", S, "int32"), ("ZRw", ZW, "float32"),
-        ("Mi", 256, "int32"), ("Tm", 256, "int32"), ("Tm2", 256, "int32"), ("Mo", 256, "float32"),
-        ("oi", 136, "int32"), ("ob", 136, "bfloat16"),
-        ("vR", 4096, "bfloat16"), ("vI", 4096, "bfloat16"), ("vN", 4096, "bfloat16"),
-        ("mxA", 2048, "bfloat16"), ("mnA", 2048, "bfloat16"), ("mxB", 2048, "bfloat16"), ("mnB", 2048, "bfloat16"),
-        ("tt", 256, "float32"), ("ti", 256, "int32"),
-        ("CR", 256, "bfloat16"), ("CI", 256, "bfloat16"), ("CB", 256, "bfloat16"),
-        ("TR", 256, "bfloat16"), ("TI", 256, "bfloat16"), ("TB", 256, "bfloat16"),
-        ("mA", 2048, "bfloat16"), ("mB", 2048, "bfloat16"), ("mC", 2048, "bfloat16"),
-        ("Fs", 512, "float32"), ("nw", 512, "float32"), ("np", 512, "float32"),
-        ("RSR", 256, "float32"), ("RSI", 512, "float32"), ("NSI", 512, "float32"), ("NSR", 512, "float32"),
-        ("MF", 256, "float32"), ("SRs", 256, "float32"), ("SIs", 256, "float32"),
-        ("rm", 256, "bfloat16"), ("RM", 256, "bfloat16"), ("ex", 256, "float32"),
-        ("nU", 256, "uint16"), ("nF", 256, "float32"), ("bG", 256, "bfloat16"), ("dm", 256, "bfloat16"),
-        ("bs", 256, "bfloat16"), ("EQ", 4096, "bfloat16"), ("fG", 256, "bfloat16"),
-        ("fd", 256, "bfloat16"), ("fs", 256, "bfloat16"), ("vS", 256, "bfloat16"), ("vT", 256, "bfloat16"),
-        ("fI", 256, "bfloat16"), ("fR", 256, "bfloat16"), ("PC", 272, "float32"),
-        ("mk2", 256, "float32"), ("DL", 256, "float32"), ("ez", 256, "float32"), ("zG", 256, "float32"),
-        ("wG", 256, "bfloat16"), ("ov", 256, "float32"), ("oq", 256, "float32"), ("ow", 256, "float32"),
-        ("wf", 256, "float32"), ("Dr", 256, "float32"), ("TH", 128, "float32"), ("TH0", 128, "float32"),
-        ("sF32", 256, "float32"), ("sI32", 64, "int32"), ("sU16", 64, "uint16"), ("pi", 4, "int32"), ("pf", 8, "float32"),
-        ("E", 2048, "bfloat16"), ("one", 2048, "bfloat16"), ("m0", 1024, "bfloat16"), ("a0", 1024, "bfloat16"),
-        ("AK", 256, "float32"), ("mkf", 256, "float32"), ("BK", 256, "bfloat16"), ("BK1", 256, "bfloat16"),
-        ("BC", 256, "bfloat16"), ("BM", 16, "bfloat16"), ("BV", 16, "bfloat16"), ("KR", 256, "bfloat16"),
-        ("Ib", 128, "bfloat16"), ("If", 128, "float32"), ("W1", 128, "bfloat16"), ("W2", 128, "bfloat16"),
-        ("W0", 128, "bfloat16"), ("thr", 256, "float32"), ("pw", 256, "float32"), ("pv", 256, "float32"),
-        ("CC", 8, "float32"), ("MI", 256, "float32"), ("MIb", 256, "bfloat16"), ("ii", 256, "float32"),
-        ("bi", 16, "int32"), ("ks", 32, "float32"), ("o6", 128, "float32"), ("B8", 128, "float32")]:
-    _d("c_" + _n, "sbuf", [128, _c], _t)
-for _k, _n in enumerate(("lR", "sF", "w1", "w2", "dc", "won", "d1", "d2", "d3", "zi", "zr", "ch")):
+for _t, _l in (
+        ("bfloat16", "Xw:2560 OWw:2560 ob:136 vR:4096 vI:4096 vN:4096 mxA:2048 mnA:2048 mxB:2048 mnB:2048 CR:256 CI:256 CB:256 "
+                     "TR:256 TI:256 TB:256 mA:2048 mB:2048 mC:2048 mD:2048 rm:256 bG:256 dm:256 bs:256 EQ:4096 fG:256 fd:256 "
+                     "fs:256 vS:256 vT:256 fI:256 fR:256 mh:128 Nb:128 BA:16 E:2048 one:256 hf:2048 m0:1024 a0:1024 BK:256 "
+                     "BK1:256 BC:256 BM:16 BV:16 KR:256 Ib:128 W1:128 W2:128 W0:128 MIb:256"),
+        ("float32", "ZRw:640 Mo:256 kR:256 thd:256 Fs:512 nw:512 np:512 RSI:512 NSI:512 NSR:512 MF:256 SIs:256 ex:256 nF:256 "
+                    "PC:272 mk2:256 DL:256 ez:256 zG:256 ov:256 ow:256 wf:256 TH:128 TH0:128 sF32:256 pf:8 AK:256 mkf:256 "
+                    "If:128 thr:256 pw:256 pv:256 CC:8 MI:256 ii:256 ks:32 o6:128 B8:128"),
+        ("int32", "NBw:2176 Mi:256 Tm:256 Tm2:256 oi:136 sI32:64 pi:4 bi:32 thi:1"),
+        ("uint16", "nU:256 sU16:64 BL:32")):
+    for _x in _l.split():
+        _d("c_" + _x.split(":")[0], "sbuf", [128, int(_x.split(":")[1])], _t)
+for _k, _n in enumerate(("sF", "w1", "w2", "dc", "won", "d1", "d2", "d3", "zi", "zr", "ch")):
     ALIAS[_n] = ("c_sF32", 16 * _k, 16)
 for _k, _n in enumerate(("wc", "w16", "thf")):
     ALIAS[_n] = ("c_sF32", 192 + 16 * _k, 1)
 for _k, (_n, _c) in enumerate((("pk", 16), ("si", 16), ("wi", 1), ("wj", 1))):
     ALIAS[_n] = ("c_sI32", 16 * _k, _c)
-_d("c_thi", "sbuf", [128, 1], "int32")
 for _k, _n in enumerate(("sU", "bU", "sWU", "bWU")):
     ALIAS[_n] = ("c_sU16", 16 * _k, 16)
-_d("c_BL", "sbuf", [128, 16], "uint16")
 for _t in range(RO):
     _d("Mu%d" % _t, "sbuf", [128, 256], "uint16")
     _d("Lin%d" % _t, "sbuf", [128, 256], "uint16")
     _d("Do%d" % _t, "sbuf", [128, 256], "float32")
     _d("Din%d" % _t, "sbuf", [128, 256], "float32")
-for _n in ("BC0", "BC1", "BC2", "KE0", "KE1", "SIT", "MS0", "MS1"):
+for _n in ("BC0", "BC1", "BC2", "BC3", "KE0", "KE1", "SIT", "MS0"):
     _d("p_" + _n, "psum", [128, 512], "float32")
 _d("ownd", "dram", [8, S], "bfloat16")
 
 SEMAPHORES = (["qV", "qS", "qP", "qG", "dx", "dm", "dn", "do", "dod", "dor", "dth", "dy", "dyo"]
-              + ["aL%d" % t for t in range(RO)] + ["aD%d" % t for t in range(RO)]
-              + ["lL%d" % t for t in range(RO)] + ["lD%d" % t for t in range(RO)])
+              + [n + "%d" % t for n in ("aL", "aD", "lL", "lD") for t in range(RO)])
 
 
 def rank_program(g, core, T, topo):
@@ -92,6 +71,9 @@ def rank_program(g, core, T, topo):
         c0 = o + c0
         ap = T[name][p0:p1, c0:c1] if st == 1 else T[name][p0:p1, c0:c1:st]
         return (ap, name, c0, c1)
+
+    def H(name, h, o=0):
+        return R(name, o + h * 128, o + h * 128 + 128)
 
     def ind(win, off):
         return win[0].indirect(off[0])
@@ -127,14 +109,14 @@ def rank_program(g, core, T, topo):
                 Q[queue].wait_ge(T.sem[src], nd[src])
                 learn(queue, src, nd[src])
 
-    def note(queue, src, n, reads, writes):
+    def note(queue, label, src, n, reads, writes):
         snap[(src, n)] = dict(known[queue])
         for regs, wr in ((reads, False), (writes, True)):
             for r in regs:
                 lst = acc.get(r[1], [])
                 if wr:
                     lst = [e for e in lst if not (e[0] >= r[2] and e[1] <= r[3])]
-                acc[r[1]] = lst + [(r[2], r[3], queue, src, n, wr)]
+                acc[r[1]] = lst + [(r[2], r[3], label, src, n, wr)]
 
     def op(queue, fn, reads, writes):
         waits(queue, need(queue, reads, writes))
@@ -142,11 +124,11 @@ def rank_program(g, core, T, topo):
         cnt[queue] += 1
         inst.then_inc(T.sem["q" + queue], 1)
         total["q" + queue] = cnt[queue]
-        note(queue, "q" + queue, cnt[queue], reads, writes)
+        note(queue, queue, "q" + queue, cnt[queue], reads, writes)
 
-    def act(out, in_, off=None):
+    def act(out, in_, off=None, func=AF.Copy):
         src = in_[0] if off is None else ind(in_, off)
-        op("S", lambda: g.scalar.activation(out[0], src, AF.Copy), [in_] + ([off] if off else []), [out])
+        op("S", lambda: g.scalar.activation(out[0], src, func), [in_] + ([off] if off else []), [out])
 
     def cp(out, in_, off=None):
         src = in_[0] if off is None else ind(in_, off)
@@ -170,8 +152,8 @@ def rank_program(g, core, T, topo):
         else:
             op("V", lambda: g.vector.tensor_scalar(out[0], a[0], x1, s2, o1, o2), rd, [out])
 
-    def scan(out, a, b, o1, o2, init=0.0):
-        op("V", lambda: g.vector.tensor_tensor_scan(out[0], a[0], b[0], init, o1, o2), [a, b], [out])
+    def scan(out, a, b, o1, o2):
+        op("V", lambda: g.vector.tensor_tensor_scan(out[0], a[0], b[0], 0.0, o1, o2), [a, b], [out])
 
     def fill(out, x):
         op("V", lambda: g.vector.memset(out[0], x), [], [out])
@@ -188,12 +170,12 @@ def rank_program(g, core, T, topo):
     def asel(out, in_, pat, cmp_, base, mult):
         op("G", lambda: g.affine_select(out[0], in_[0], pat, cmp_, 0.0, base, mult), [in_], [out])
 
-    def dma(sem, pairs, reads, writes):
-        waits("Y", need("Y", reads, writes))
+    def dma(sem, pairs, reads, writes, queue="Y"):
+        waits(queue, need(queue, reads, writes))
         for o, i in pairs:
-            g.sync.dma_start(o, i).then_inc(T.sem[sem], 16)
+            Q[queue].dma_start(o, i).then_inc(T.sem[sem], 16)
         total[sem] = 16 * len(pairs)
-        note("Y", sem, total[sem], reads, writes)
+        note(queue, "D", sem, total[sem], reads, writes)
 
     def send(buf, land, dst, asem, lsem):
         eng = topo.engines(core, dst)[:8]
@@ -210,14 +192,15 @@ def rank_program(g, core, T, topo):
         total[asem] = n
         acc[land] = [(0, 256, "X", asem, n, True)]
 
-    dma("dm", [(T.c_Mi[:, :], T.m0[:, :])], [], [R("Mi")])
+    dma("dm", [(T.c_Mi[:, :], T.m0[:, :])], [], [R("Mi")], "S")
     dma("dx", [(T.c_Xw[:, 0:S], T.x0[:, :])], [], [R("Xw", 0, S)])
     dma("do", [(T.c_oi[:, :], T.own0[:, :])], [], [R("oi")])
     dma("dth", [(T.c_thi[0:8, :], T.th[:, :])], [], [R("thi", 0, 1)])
     dma("dn", [(T.c_NBw[:, :], T.nb[:, :])], [], [R("NBw")])
+    fill(R("one"), 1.0)
     fill(R("m0"), 1.0)
     fill(R("a0"), 0.0)
-    fill(R("one"), 1.0)
+    fill(R("hf"), 0.5)
     fill(R("m0", 0, 1024, 16), 0.0)
     fill(R("a0", 0, 1024, 16), 512.0)
     cp(R("Mu0"), R("Mi"))
@@ -225,10 +208,11 @@ def rank_program(g, core, T, topo):
         arrive("Lin%d" % t, "aL%d" % t, T.cores[(rank - 1 - t) % N])
         arrive("Din%d" % t, "aD%d" % t, T.cores[(rank + 1 + t) % N])
     iota(R("pi", 0, 1), [[0, 1]], 0, 1)
-    iota(R("bi"), [[1, 16]], 0, 0)
+    iota(R("bi", 0, 16), [[1, 16]], 0, 0)
+    iota(R("bi", 16, 32), [[16, 16]], 15, 0)
     asel(R("Ib"), R("one", 0, 128), [[-1, 128]], OP.is_equal, 0, 1)
     send(R("Mu0"), "Lin0", T.cores[(rank + 1) % N], "aL0", "lL0")
-    asel(R("E"), R("one"), [[-1, 128], [0, 16]], OP.is_equal, 0, 1)
+    asel(R("E"), R("hf"), [[-1, 128], [0, 16]], OP.is_equal, 0, 1)
     asel(R("BK1"), R("one", 0, 256), [[0, 2], [-16, 8], [0, 16]], OP.is_ge, 0, 1)
     asel(R("BK"), R("BK1"), [[0, 2], [16, 8], [0, 16]], OP.is_ge, 15, -1)
     iota(R("KR"), [[-15, 2], [0, 8], [1, 16]], 0, 0)
@@ -241,10 +225,11 @@ def rank_program(g, core, T, topo):
         dma("dod", [(T.ownd[:, :], T.c_ob[:, :])], [R("ob")], [("", "ownd", 0, S)])
         dma("dor", [(T.c_OWw[i::16, 0:S], T.ownd[:, :]) for i in range(16)], [("", "ownd", 0, S)], [R("OWw", 0, S)])
         ts(R("pi", 1, 2), R("pi", 0, 1), 15, OP.bitwise_and)
-        cp(R("pf", 0, 1), R("pi", 1, 2))
-        ts(R("pf", 1, 2), R("pf", 0, 1), 1.0, OP.add, 4096.0, OP.mult)
-        ts(R("MF"), R("Mu0"), R("pf", 1, 2), OP.add)
         cp(R("If"), R("Ib"))
+        cp(R("pf", 0, 1), R("pi", 1, 2))
+        ts(R("Nb"), R("Ib"), -1.0, OP.mult)
+        ts(R("pf", 1, 2), R("pf", 0, 1), 1.0, OP.add, 4096.0, OP.mult)
+        fill(R("mh"), -0.5)
         cp(R("BL"), R("bi"))
 
     def consts_mid():
@@ -252,167 +237,175 @@ def rank_program(g, core, T, topo):
         ts(R("BM", 8, 16), R("BK", 0, 128, 16), -32.0, OP.mult)
         ts(R("BV", 0, 8), R("BK", 0, 128, 16), -16.0, OP.mult)
         ts(R("BV", 8, 16), R("BK", 0, 128, 16), 16.0, OP.mult)
-        ts(R("BC", 0, 128), R("BK", 0, 128), -16.0, OP.mult)
-        ts(R("BC", 128, 256), R("BK", 0, 128), 16.0, OP.mult)
+        ts(R("BC", 0, 128), R("BK", 0, 128), -8.0, OP.mult)
+        ts(R("BC", 128, 256), R("BK", 0, 128), 8.0, OP.mult)
+        ts(R("BA"), R("BV"), -1.0, OP.mult)
         fill(R("AK"), 0.0)
         fill(R("mkf"), 1.0)
+        ts(R("MI"), R("ii"), R("pf", 0, 1), OP.is_equal)
         fill(R("AK", 0, 256, 16), 1000000.0)
         fill(R("mkf", 0, 256, 16), 0.0)
-        ts(R("MI"), R("ii"), R("pf", 0, 1), OP.is_equal)
         cp(R("MIb"), R("MI"))
         cp(R("CC"), R("BK", 0, 128, 16))
 
     def consts_late():
         fill(R("pw"), 0.0)
-        fill(R("pw", 0, 256, 16), 2.0)
         ts(R("pv"), R("mkf"), 0.5, OP.mult)
+        fill(R("pw", 0, 256, 16), 2.0)
         scan(R("thr"), R("pv"), R("pw"), OP.mult, OP.add)
-        tt(R("wf", 0, 16), R("thr", 0, 16), R("MI", 0, 16), OP.mult)
-        rsum(R("pf", 2, 3), R("wf", 0, 16))
+        fill(R("W0"), 0.0)
+        tt(R("thd"), R("thr"), R("MI"), OP.mult)
+        fill(R("o6"), 0.0625)
+        rsum(R("pf", 2, 3), R("thd", 0, 16))
         ts(R("W1"), R("BK", 0, 128), 64.0, OP.mult)
         ts(R("W2"), R("BK", 0, 128), R("pf", 2, 3), OP.mult, 0.5, OP.mult)
-        fill(R("W0"), 0.0)
-        fill(R("o6"), 0.0625)
         fill(R("PC", 0, 16), 0.0)
         cp(R("thf", 0, 1, 1, 0, 8), R("thi", 0, 1, 1, 0, 8))
-        ts(R("B8", 0, 128, 1, 0, 8), R("E", 0, 128, 1, 0, 8), R("thf", 0, 1, 1, 0, 8), OP.mult, 256.0, OP.mult)
-        mm(R("MS1", 0, 128), R("o6", 0, 128, 1, 0, 8), R("B8", 0, 128, 1, 0, 8))
-        cp(R("TH0"), R("MS1", 0, 128))
+        ts(R("B8", 0, 128, 1, 0, 8), R("E", 0, 128, 1, 0, 8), R("thf", 0, 1, 1, 0, 8), OP.mult, 512.0, OP.mult)
+        mm(R("MS0", 0, 128), R("o6", 0, 128, 1, 0, 8), R("B8", 0, 128, 1, 0, 8))
+        cp(R("TH0"), R("MS0", 0, 128))
 
     def gather(v, lst, h):
         for c in range(2):
             a = h * 128 + c * 64
             act(R(v, a * 16, a * 16 + 1024), R("Xw", 0, S), R(lst, a, a + 64))
 
-    def scans(v, h, C, bufs):
+    def scans(v, h, bufs, nat):
         mx, mn = bufs
         for c in range(2):
             x = R(v, h * 2048 + c * 1024, h * 2048 + c * 1024 + 1024)
             scan(R(mx, c * 1024, c * 1024 + 1024), R("m0"), x, OP.mult, OP.max)
             scan(R(mn, c * 1024, c * 1024 + 1024), R("a0"), x, OP.add, OP.min)
-        a, b = h * 128, h * 128 + 128
-        tt(R("tt", a, b), R(mx, 15, 2048, 16), R(mn, 15, 2048, 16), OP.add)
-        ts(R("ti", a, b), R("tt", a, b), 0.5, OP.mult, -0.25, OP.add)
-        cp(R(C, a, b), R("ti", a, b))
+        a, b = R(mx, 15, 2048, 16), R(mn, 15, 2048, 16)
+        one, mh = R("one", 0, 128, 1, 0, 1), R("mh", 0, 128, 1, 0, 1)
+        mm(H("MS0", h), a, R("Ib"), True, False)
+        mm(H("MS0", h), b, R("Ib"), False, False)
+        mm(H("MS0", h), one, mh, False, True)
+        if nat:
+            mm(H("MS0", h, 256), R("Ib"), a, True, False)
+            mm(H("MS0", h, 256), R("Ib"), b, False, False)
+            mm(H("MS0", h, 256), one, mh, False, True)
 
-    def turn(C, h):
-        mm(R("MS0", h * 128, h * 128 + 128), R(C, h * 128, h * 128 + 128), R("Ib"))
+    def floor2(out, h, o=0):
+        ts(H(out, h), H("MS0", h, o), 16777216.0, OP.add, 16777216.0, OP.subtract)
 
-    def turned(TC, h):
-        cp(R(TC, h * 128, h * 128 + 128), R("MS0", h * 128, h * 128 + 128))
-
-    bcn, ken, mbn, bank = [0], [0], [0], {}
+    bcn, ken, mbn, bank, kes = [0], [0], [0], {}, {}
 
     def bc(u, b):
-        k = "BC%d" % (bcn[0] % 3)
+        k = "BC%d" % (bcn[0] % 4)
         bcn[0] += 1
         bank[(u, b)] = k
-        mm(R(k), R(u[2], u[4] * 128, u[4] * 128 + 128), R("E", b * 512, b * 512 + 512))
+        mm(R(k), H(u[2], u[4]), R("E", b * 512, b * 512 + 512), True, u[3] is not None)
+        if u[3] is None:
+            mm(R(k), R("Nb"), R(u[1], u[4] * 2048 + b * 512, u[4] * 2048 + b * 512 + 512), False, True)
 
-    def run_units(units, after):
+    def key(u, mb):
+        ke = "KE%d" % (ken[0] % 2)
+        ken[0] += 1
+        h = u[4]
+        mm(R(ke, 0, 256), R("one", 0, 128, 1, 0, 1), R("KR", 0, 256, 1, 0, 1), True, False)
+        if u[3] is not None:
+            mm(R(ke, 0, 256), H(u[3], h), R("BC"), False, False)
+            for k in range(16):
+                mm(R(ke, k, 256, 16), R(u[1], h * 2048 + k, h * 2048 + 2048, 16), R("BV"), False, False)
+        for k in range(16):
+            mm(R(ke, k, 256, 16), R(mb, k, 2048, 16), R("BM" if u[3] is not None else "BA"), False, k == 15)
+        kes[(u[0], h)] = ke
+
+    def run_units(units, hooks={}):
         flat = [(u, b) for u in units for b in range(4)]
-        for u, b in flat[:3]:
+        for u, b in flat[:4]:
             bc(u, b)
         for n, (u, b) in enumerate(flat):
             if b == 0:
-                mb = "m" + "ABC"[mbn[0] % 3]
+                mb = "m" + "ABCD"[mbn[0] % 4]
                 mbn[0] += 1
-            x = R(u[1], u[4] * 2048 + b * 512, u[4] * 2048 + b * 512 + 512)
-            tt(R(mb, b * 512, b * 512 + 512), x, R(bank[(u, b)]), OP.max)
-            if n + 3 < len(flat):
-                bc(*flat[n + 3])
+            o = R(mb, b * 512, b * 512 + 512)
+            if u[3] is None:
+                act(o, R(bank[(u, b)]), None, AF.Abs)
+            else:
+                tt(o, R(u[1], u[4] * 2048 + b * 512, u[4] * 2048 + b * 512 + 512), R(bank[(u, b)]), OP.max)
+            if n + 4 < len(flat):
+                bc(*flat[n + 4])
             if b == 3:
-                ke = "KE%d" % (ken[0] % 2)
-                ken[0] += 1
-                h = u[4]
-                mm(R(ke, 0, 256), R("one", 0, 128, 1, 0, 1), R("KR", 0, 256, 1, 0, 1), True, False)
-                mm(R(ke, 0, 256), R(u[3], h * 128, h * 128 + 128), R("BC"), False, False)
-                for k in range(16):
-                    mm(R(ke, k, 256, 16), R(u[1], h * 2048 + k, h * 2048 + 2048, 16), R("BV"), False, False)
-                for k in range(16):
-                    mm(R(ke, k, 256, 16), R(mb, k, 2048, 16), R("BM"), False, k == 15)
-                after(u, ke)
+                key(u, mb)
+                if u in hooks:
+                    hooks[u]()
 
-    def pick(ke, res, h, sit, xs, wide):
-        for x in xs:
-            k = R(ke, x * 128, x * 128 + 128)
-            o = x * 128
-            scan(R("Fs", o, o + 128), R("AK", 0, 128), k, OP.add, OP.min)
-            tt(R("nw", o, o + 128), k, R("Fs", o, o + 128), OP.is_equal)
-            tt(R("np", o, o + 128), R("nw", o, o + 128), R(sit, h * 128, h * 128 + 128), OP.mult)
-            d = (x * 256 if wide else 0) + h * 128
-            scan(R(res, d, d + 128), R("mkf", 0, 128), R("np", o, o + 128), OP.mult, OP.max)
+    def pick(jobs):
+        jobs = [(H(kes[(who, h)], x), H(res, 2 * x + h), h, n) for n, (who, res, h, x) in enumerate(jobs)]
+        for k, res, h, n in jobs:
+            scan(H("Fs", n), R("AK", 0, 128), k, OP.add, OP.min)
+        for k, res, h, n in jobs:
+            tt(H("nw", n), k, H("Fs", n), OP.is_equal)
+        for k, res, h, n in jobs:
+            tt(H("np", n), H("nw", n), H("SIT", h), OP.mult)
+        for k, res, h, n in jobs:
+            scan(res, R("mkf", 0, 128), H("np", n), OP.mult, OP.max)
 
     def flip(src, ps, idn):
         for h in range(2):
-            mm(R(ps, h * 128, h * 128 + 128), R(src, h * 128, h * 128 + 128), R(idn))
+            mm(H(ps, h), H(src, h), R(idn))
 
+    E16 = (15, 256, 16)
+    E16b = (271, 512, 16)
+    BL = R("BL", 0, 16)
     for t in range(RO):
         last = t == RO - 1
         mu, li, do = "Mu%d" % t, "Lin%d" % t, "Do%d" % t
-        kes = {}
-
-        def after(u, ke):
-            kes[(u[0], u[4])] = ke
-
         gather("vR", mu, 0)
         gather("vR", mu, 1)
         if t == 0:
             consts_early()
-        else:
-            ts(R("MF"), R(mu), R("pf", 1, 2), OP.add)
-        scans("vR", 0, "CR", ("mxA", "mnA"))
-        turn("CR", 0)
-        flip("MF", "SIT", "If")
+        scans("vR", 0, ("mxA", "mnA"), True)
         if t == 0:
             consts_mid()
-        scans("vR", 1, "CR", ("mxB", "mnB"))
-        turned("TR", 0)
-        turn("CR", 1)
+        scans("vR", 1, ("mxB", "mnB"), True)
+        floor2("TR", 0)
+        floor2("CR", 0, 256)
         gather("vI", li, 0)
         gather("vI", li, 1)
-        act(R("SRs"), R("SIT", 0, 256))
-        turned("TR", 1)
-        run_units([("R", "vR", "TR", "CR", 0), ("R", "vR", "TR", "CR", 1)], after)
+        floor2("TR", 1)
+        floor2("CR", 1, 256)
+        run_units([("R", "vR", "TR", "CR", 0), ("R", "vR", "TR", "CR", 1)])
         ts(R("MF"), R(li), R("pf", 1, 2), OP.add)
-        flip("MF", "MS1", "If")
-        scans("vI", 0, "CI", ("mxA", "mnA"))
-        pick(kes[("R", 0)], "RSR", 0, "SIT", [1], False)
-        turn("CI", 0)
-        pick(kes[("R", 1)], "RSR", 1, "SIT", [1], False)
-        scans("vI", 1, "CI", ("mxB", "mnB"))
-        turned("TI", 0)
-        turn("CI", 1)
-        act(R("SIs"), R("MS1", 0, 256))
-        cp(R("lR"), R("RSR", 15, 256, 16))
-        turned("TI", 1)
-        run_units([("I", "vI", "TI", "CI", 0), ("I", "vI", "TI", "CI", 1)], after)
-        tt(R("rm"), R("lR"), R("SRs"), OP.is_equal, R("BL"))
-        pick(kes[("I", 0)], "RSI", 0, "MS1", [0], True)
-        pick(kes[("I", 1)], "RSI", 1, "MS1", [0], True)
-        cp(R("pk"), R("RSI", 15, 256, 16))
-        ts(R("si"), R("pk"), 4095, OP.bitwise_and)
-        tt(R("ex"), R("si"), R("MI"), OP.mult, R("BL"))
+        flip("MF", "SIT", "If")
+        scans("vI", 0, ("mxA", "mnA"), False)
+        floor2("TI", 0)
         for h in range(2):
-            mm(R("MS0", h * 8, h * 8 + 8), R("ex", h * 128, h * 128 + 128), R("CC"))
+            scan(H("Fs", h), R("AK", 0, 128), H(kes[("R", h)], 1), OP.add, OP.min)
+            cp(H("kR", h), H(kes[("R", h)], 1))
+        run_units([("I", "vI", "TI", None, 0)])
+        scans("vI", 1, ("mxB", "mnB"), True)
+        act(R("SIs"), R("SIT", 0, 256))
+        tt(R("rm"), R("Fs", 0, 256), R("kR"), OP.is_equal, R("BL", 16, 32))
+        floor2("TI", 1)
+        floor2("CI", 1, 256)
+        run_units([("I", "vI", "TI", "CI", 1)])
+        pick([("I", "RSI", 0, 0), ("I", "RSI", 1, 0)])
+        cp(R("pk"), R("RSI", *E16))
+        ts(R("si"), R("pk"), 4095, OP.bitwise_and)
+        tt(R("ex"), R("si"), R("MI"), OP.mult, BL)
+        for h in range(2):
+            mm(R("MS0", h * 8, h * 8 + 8), H("ex", h), R("CC"))
         cp(R("sU"), R("MS0", 0, 16))
         cp(R("nU"), R("NBw"), R("sU"))
-        for c in range(4):
-            act(R("vN", c * 1024, c * 1024 + 1024), R("Xw", 0, S), R("nU", c * 64, c * 64 + 64))
-        cp(R("sF"), R("sU"))
+        for h in range(2):
+            gather("vN", "nU", h)
+        tt(R("dm"), R("OWw", 0, S), R("MIb"), OP.mult, R("sU"))
         cp(R("bG"), R("OWw", 0, S), R("sU"))
-        tt(R("dm"), R("bG"), R("MIb"), OP.mult)
         scan(R("bs"), R("m0", 0, 256), R("dm"), OP.mult, OP.add)
-        cp(R("bU"), R("bs", 15, 256, 16))
+        cp(R("sF"), R("sU"))
+        cp(R("bU"), R("bs", *E16))
         cp(R("CB"), R("CR"), R("bU"))
         for h in range(2):
-            turn("CB", h)
+            mm(H("MS0", h), H("CB", h), R("Ib"))
+        pick([("I", "RSI", 0, 1), ("I", "RSI", 1, 1)])
         for h in range(2):
-            pick(kes[("I", h)], "RSI", h, "MS1", [1], True)
-        for h in range(2):
-            turned("TB", h)
+            cp(H("TB", h), H("MS0", h))
         ts(R("nF"), R("nU"), R("pf", 1, 2), OP.add)
         flip("nF", "SIT", "If")
+        th = "TH"
         if t == 0:
             consts_late()
             th = "TH0"
@@ -422,88 +415,94 @@ def rank_program(g, core, T, topo):
             ts(R("wj"), R("wi"), 63, OP.bitwise_and)
             ts(R("w16"), R("wj"), 16.0, OP.mult)
             ts(R("TH"), R("TH0"), R("w16"), OP.add)
-            th = "TH"
 
         def judge(who, h):
-            ke, intr = kes[(who, h)], who == "NI"
-            pick(ke, "NSI" if intr else "NSR", h, "SIT", [0, 1], True)
-            tt(R("fI" if intr else "fR", h * 128, h * 128 + 128), R(ke, 0, 128), R(th), OP.is_lt)
+            res = "NSI" if who == "NI" else "NSR"
+            tt(H("fI" if who == "NI" else "fR", h), H(kes[(who, h)], 0), R(th), OP.is_lt)
+            pick([(who, res, h, 0), (who, res, h, 1)])
 
-        run_units([("NI", "vN", "TI", "CI", 0), ("NR", "vN", "TB", "CB", 0)], after)
+        run_units([("NR", "vN", "TB", "CB", 0)])
         offs = [sum(256 - 16 * x for x in range(c)) for c in range(16)]
         for c in range(16):
             ts(R("EQ", offs[c], offs[c] + 256 - 16 * c), R("bG", 16 * c, 256), R("bs", 16 * c + 15, 16 * c + 16), OP.is_equal)
-        mm(R("MS1", 0, 256), R("W0"), R("EQ", 0, 256), True, False)
+        mm(R("MS0", 0, 256), R("W0"), R("EQ", 0, 256), True, False)
         for c in range(16):
             if c < 15:
-                mm(R("MS1", 16 * c + 16, 256), R("W1"), R("EQ", offs[c] + 16, offs[c] + 256 - 16 * c), False, False)
-            mm(R("MS1", 16 * c, 16 * c + 16), R("W2"), R("EQ", offs[c], offs[c] + 16), False, c == 15)
-        judge("NI", 0)
+                mm(R("MS0", 16 * c + 16, 256), R("W1"), R("EQ", offs[c] + 16, offs[c] + 256 - 16 * c), False, False)
+            mm(R("MS0", 16 * c, 16 * c + 16), R("W2"), R("EQ", offs[c], offs[c] + 16), False, c == 15)
         judge("NR", 0)
-        tt(R("fG"), R("MS1", 0, 256), R("thr"), OP.is_lt)
-        run_units([("NI", "vN", "TI", "CI", 1), ("NR", "vN", "TB", "CB", 1)], after)
-        flip("rm", "MS0", "Ib")
-        act(R("RM"), R("MS0", 0, 256))
-        tt(R("fd"), R("fG"), R("MIb"), OP.mult)
-        scan(R("fs"), R("m0", 0, 256), R("fd"), OP.mult, OP.add)
-        tt(R("w1"), R("sF"), R("ks", 0, 16), OP.subtract)
-        tt(R("w2"), R("bs", 15, 256, 16), R("ks", 16, 32), OP.subtract)
-        tt(R("w1"), R("w1"), R("fs", 15, 256, 16), OP.mult)
-        tt(R("w2"), R("w2"), R("fs", 15, 256, 16), OP.mult)
-        tt(R("w1"), R("w1"), R("ks", 0, 16), OP.add)
-        tt(R("w2"), R("w2"), R("ks", 16, 32), OP.add)
-        cp(R("sWU"), R("w1"))
-        cp(R("bWU"), R("w2"))
+        tt(R("fd"), R("MS0", 0, 256), R("thd"), OP.is_lt)
+        tt(R("fG"), R("MS0", 0, 256), R("thr"), OP.is_lt)
+
+        def lists():
+            scan(R("fs"), R("m0", 0, 256), R("fd"), OP.mult, OP.add)
+            tt(R("w1"), R("sF"), R("ks", 0, 16), OP.subtract)
+            tt(R("w2"), R("bs", *E16), R("ks", 16, 32), OP.subtract)
+            tt(R("w1"), R("w1"), R("fs", *E16), OP.mult)
+            tt(R("w2"), R("w2"), R("fs", *E16), OP.mult)
+            tt(R("w1"), R("w1"), R("ks", 0, 16), OP.add)
+            tt(R("w2"), R("w2"), R("ks", 16, 32), OP.add)
+            cp(R("sWU"), R("w1"))
+            cp(R("bWU"), R("w2"))
+            fill(R("ZRw", 0, 256), 0.0)
+            tt(R("d3"), R("RSI", *E16b), R("RSI", *E16), OP.subtract)
+            if not last:
+                cp(R("vS"), R("Xw", 0, S), R("sU"))
+                ts(R("vT"), R("vS"), -8.0, OP.add, 0.0, OP.max)
+
+        ni0, ni1 = ("NI", "vN", "TI", None, 0), ("NI", "vN", "TI", None, 1)
+        run_units([ni0, ni1, ("NR", "vN", "TB", None, 1)], {ni0: lists, ni1: lambda: judge("NI", 0)})
         judge("NI", 1)
-        if not last:
-            cp(R("vS"), R("Xw", 0, S), R("sU"))
-            ts(R("vT"), R("vS"), -8.0, OP.add, 0.0, OP.max)
-        tt(R("d3"), R("RSI", 271, 512, 16), R("RSI", 15, 256, 16), OP.subtract)
         judge("NR", 1)
+        flip("rm", "SIT", "Ib")
         scan(R("PC", 16, 272), R("fI"), R("fR"), OP.add, OP.subtract)
-        tt(R("dc"), R("PC", 31, 272, 16), R("PC", 15, 256, 16), OP.subtract)
+        tt(R("d1"), R("NSI", *E16), R("NSR", *E16b), OP.subtract)
+        tt(R("dc"), R("PC", 31, 272, 16), R("PC", *E16), OP.subtract)
+        tt(R("d2"), R("NSI", *E16b), R("NSR", *E16), OP.subtract)
         ts(R("won"), R("dc"), 0.0, OP.is_gt)
-        tt(R("d1"), R("NSI", 15, 256, 16), R("NSR", 271, 512, 16), OP.subtract)
-        tt(R("d1"), R("d1"), R("won"), OP.mult)
-        tt(R("zi"), R("d1"), R("NSR", 271, 512, 16), OP.add)
-        tt(R("d3"), R("d3"), R("won"), OP.mult)
-        tt(R("ch"), R("d3"), R("RSI", 15, 256, 16), OP.add)
-        tt(R("mk2"), R("ch"), R("SIs"), OP.is_equal, R("BL"))
-        tt(R("DL"), R("zi"), R("mk2"), OP.mult, R("BL"))
-        flip("DL", "MS0", "If")
-        tt(R("d2"), R("NSI", 271, 512, 16), R("NSR", 15, 256, 16), OP.subtract)
         ts(R("d2"), R("d2"), 262144.0, OP.add)
+        tt(R("d3"), R("d3"), R("won"), OP.mult)
+        tt(R("d1"), R("d1"), R("won"), OP.mult)
+        tt(R("ch"), R("d3"), R("RSI", *E16), OP.add)
+        tt(R("zi"), R("d1"), R("NSR", *E16b), OP.add)
+        tt(R("mk2"), R("ch"), R("SIs"), OP.is_equal, BL)
+        tt(R("DL"), R("zi"), R("mk2"), OP.mult, BL)
+        flip("DL", "MS0", "If")
         tt(R("d2"), R("d2"), R("won"), OP.mult)
-        tt(R("zr"), R("d2"), R("NSR", 15, 256, 16), OP.add)
-        act(R("ez"), R("zr"), R("BL"))
-        flip("ez", "MS1", "If")
+        tt(R("zr"), R("d2"), R("NSR", *E16), OP.add)
+        act(R("ez"), R("zr"), BL)
+        flip("ez", "BC0", "If")
         tt(R(do), R("MS0", 0, 256), R("fG"), OP.mult)
         send(R(do), "Din%d" % t, T.cores[(rank - 1 - t) % N], "aD%d" % t, "lD%d" % t)
-        act(R("zG"), R("MS1", 0, 256))
-        fill(R("ZRw", 0, 256), 0.0)
+        act(R("zG"), R("BC0", 0, 256))
         if not last:
             scat(R("Xw"), R("sWU"), R("vT"))
         scat(R("ZRw"), R("bWU"), R("zG"))
-        tt(R("Dr"), R("ZRw", 0, 256), R("RM"), OP.mult)
-        tt(R("Tm"), R("Mi"), R("Dr"), OP.max)
-        ts(R("wG"), R("zG"), 262144.0, OP.is_ge)
-        tt(R("ov"), R("bG"), R("wG"), OP.add)
-        ts(R("oq"), R("ov"), 256.0, OP.is_ge, -256.0, OP.mult)
-        tt(R("ow"), R("ov"), R("oq"), OP.add)
-        scat(R("OWw"), R("sWU"), R("ow"))
+        tt(R("SIT", 256, 512), R("ZRw", 0, 256), R("SIT", 0, 256), OP.mult)
+        tt(R("Tm"), R("Mi"), R("SIT", 256, 512), OP.max)
+        ts(R("Tm2"), R("Tm"), 4095, OP.bitwise_and)
+        cp(R("SIT", 0, 256), R("Tm2"))
+
+        def owners():
+            ts(R("BC1", 0, 256), R("zG"), 262144.0, OP.is_ge)
+            tt(R("ov"), R("bG"), R("BC1", 0, 256), OP.add)
+            ts(R("BC1", 256, 512), R("ov"), 256.0, OP.is_ge, -256.0, OP.mult)
+            tt(R("ow"), R("ov"), R("BC1", 256, 512), OP.add)
+            scat(R("OWw"), R("sWU"), R("ow"))
+
         if last:
+            owners()
             waits("G", need("G", [R("OWw", 0, S)], []))
             g.dma_start(T.yown[:, :], T.c_OWw[0::16, 0:S]).then_inc(T.sem.dyo, 16)
             total["dyo"] = 16
-        else:
-            tt(R("wf"), R("wG"), R("fG"), OP.mult)
-            rsum(R("wc"), R("wf"))
-        ts(R("Tm2"), R("Tm"), 4095, OP.bitwise_and)
-        tt(R("Tm"), R("Tm2"), R("Din%d" % t), OP.max)
+        tt(R("Tm"), R("Din%d" % t), R("SIT", 0, 256), OP.max)
         ts(R("Mi"), R("Tm"), 4095, OP.bitwise_and)
         if not last:
             cp(R("Mu%d" % (t + 1)), R("Mi"))
             send(R("Mu%d" % (t + 1)), "Lin%d" % (t + 1), T.cores[(rank + 2 + t) % N], "aL%d" % (t + 1), "lL%d" % (t + 1))
+            owners()
+            tt(R("wf"), R("BC1", 0, 256), R("fG"), OP.mult)
+            rsum(R("wc"), R("wf"))
         else:
             cp(R("Mo"), R("Mi"))
             dma("dy", [(T.ym[:, :], T.c_Mo[:, :])], [R("Mo")], [])

@@ -1,8 +1,6 @@
 from concourse.mybir import dt, AluOpType, AxisListType, ActivationFunctionType
 
 S, L, RO = 2176, 256, 3
-SW = 2560
-ZW = 640
 OP = AluOpType
 AF = ActivationFunctionType
 
@@ -19,7 +17,7 @@ for _t, _l in (
                      "TR:256 TI:256 TB:256 mA:2048 mB:2048 mC:2048 mD:2048 rm:256 bG:256 dm:256 bs:256 EQ:4096 fG:256 fd:256 "
                      "fs:256 vS:256 vT:256 fI:256 fR:256 mh:128 Nb:128 BA:16 E:2048 one:256 hf:2048 m0:1024 a0:1024 BK:256 "
                      "BK1:256 BC:256 BM:16 BV:16 KR:256 Ib:128 W1:128 W2:128 W0:128 MIb:256"),
-        ("float32", "ZRw:640 Mo:256 kR:256 thd:256 Fs:512 nw:512 np:512 RSI:512 NSI:512 NSR:512 MF:256 SIs:256 ex:256 nF:256 "
+        ("float32", "ZRw:640 Mo:256 kR:256 FR:256 thd:256 Fs:512 nw:512 np:512 RSI:512 NSI:512 NSR:512 MF:256 SIs:256 ex:256 nF:256 "
                     "PC:272 mk2:256 DL:256 ez:256 zG:256 ov:256 ow:256 wf:256 TH:128 TH0:128 sF32:256 pf:8 AK:256 mkf:256 "
                     "If:128 thr:256 pw:256 pv:256 CC:8 MI:256 ii:256 ks:32 o6:128 B8:128"),
         ("int32", "NBw:2176 Mi:256 Tm:256 Tm2:256 oi:136 sI32:64 pi:4 bi:32 thi:1"),
@@ -192,6 +190,13 @@ def rank_program(g, core, T, topo):
         total[asem] = n
         acc[land] = [(0, 256, "X", asem, n, True)]
 
+    def weave(*gens):
+        gens = list(gens)
+        while gens:
+            for x in list(gens):
+                if next(x, 0) == 0:
+                    gens.remove(x)
+
     dma("dm", [(T.c_Mi[:, :], T.m0[:, :])], [], [R("Mi")], "S")
     dma("dx", [(T.c_Xw[:, 0:S], T.x0[:, :])], [], [R("Xw", 0, S)])
     dma("do", [(T.c_oi[:, :], T.own0[:, :])], [], [R("oi")])
@@ -289,7 +294,7 @@ def rank_program(g, core, T, topo):
     def floor2(out, h, o=0):
         ts(H(out, h), H("MS0", h, o), 16777216.0, OP.add, 16777216.0, OP.subtract)
 
-    bcn, ken, mbn, bank, kes = [0], [0], [0], {}, {}
+    bcn, ken, mbn, bank, kes, mbs = [0], [0], [0], {}, {}, {}
 
     def bc(u, b):
         k = "BC%d" % (bcn[0] % 4)
@@ -299,10 +304,10 @@ def rank_program(g, core, T, topo):
         if u[3] is None:
             mm(R(k), R("Nb"), R(u[1], u[4] * 2048 + b * 512, u[4] * 2048 + b * 512 + 512), False, True)
 
-    def key(u, mb):
+    def key(u):
         ke = "KE%d" % (ken[0] % 2)
         ken[0] += 1
-        h = u[4]
+        h, mb = u[4], mbs[u]
         mm(R(ke, 0, 256), R("one", 0, 128, 1, 0, 1), R("KR", 0, 256, 1, 0, 1), True, False)
         if u[3] is not None:
             mm(R(ke, 0, 256), H(u[3], h), R("BC"), False, False)
@@ -316,32 +321,32 @@ def rank_program(g, core, T, topo):
         flat = [(u, b) for u in units for b in range(4)]
         for u, b in flat[:4]:
             bc(u, b)
+        if 0 in hooks:
+            hooks[0]()
         for n, (u, b) in enumerate(flat):
             if b == 0:
-                mb = "m" + "ABCD"[mbn[0] % 4]
+                mbs[u] = "m" + "ABCD"[mbn[0] % 4]
                 mbn[0] += 1
-            o = R(mb, b * 512, b * 512 + 512)
+            o = R(mbs[u], b * 512, b * 512 + 512)
             if u[3] is None:
                 act(o, R(bank[(u, b)]), None, AF.Abs)
             else:
                 tt(o, R(u[1], u[4] * 2048 + b * 512, u[4] * 2048 + b * 512 + 512), R(bank[(u, b)]), OP.max)
             if n + 4 < len(flat):
                 bc(*flat[n + 4])
-            if b == 3:
-                key(u, mb)
-                if u in hooks:
-                    hooks[u]()
+            if b == 3 and u in hooks:
+                hooks[u]()
 
     def pick(jobs):
         jobs = [(H(kes[(who, h)], x), H(res, 2 * x + h), h, n) for n, (who, res, h, x) in enumerate(jobs)]
         for k, res, h, n in jobs:
-            scan(H("Fs", n), R("AK", 0, 128), k, OP.add, OP.min)
+            yield scan(H("Fs", n), R("AK", 0, 128), k, OP.add, OP.min)
         for k, res, h, n in jobs:
-            tt(H("nw", n), k, H("Fs", n), OP.is_equal)
+            yield tt(H("nw", n), k, H("Fs", n), OP.is_equal)
         for k, res, h, n in jobs:
-            tt(H("np", n), H("nw", n), H("SIT", h), OP.mult)
+            yield tt(H("np", n), H("nw", n), H("SIT", h), OP.mult)
         for k, res, h, n in jobs:
-            scan(res, R("mkf", 0, 128), H("np", n), OP.mult, OP.max)
+            yield scan(res, R("mkf", 0, 128), H("np", n), OP.mult, OP.max)
 
     def flip(src, ps, idn):
         for h in range(2):
@@ -353,6 +358,11 @@ def rank_program(g, core, T, topo):
     for t in range(RO):
         last = t == RO - 1
         mu, li, do = "Mu%d" % t, "Lin%d" % t, "Do%d" % t
+        r0, r1 = ("R", "vR", "TR", None, 0), ("R", "vR", "TR", None, 1)
+        i0, i1 = ("I", "vI", "TI", None, 0), ("I", "vI", "TI", "CI", 1)
+        ni0, ni1 = ("NI", "vN", "TI", None, 0), ("NI", "vN", "TI", None, 1)
+        nr0, nr1 = ("NR", "vN", "TB", "CB", 0), ("NR", "vN", "TB", None, 1)
+        th = "TH" if t else "TH0"
         gather("vR", mu, 0)
         gather("vR", mu, 1)
         if t == 0:
@@ -367,93 +377,102 @@ def rank_program(g, core, T, topo):
         gather("vI", li, 1)
         floor2("TR", 1)
         floor2("CR", 1, 256)
-        run_units([("R", "vR", "TR", "CR", 0), ("R", "vR", "TR", "CR", 1)])
         ts(R("MF"), R(li), R("pf", 1, 2), OP.add)
         flip("MF", "SIT", "If")
         scans("vI", 0, ("mxA", "mnA"), False)
         floor2("TI", 0)
-        for h in range(2):
-            scan(H("Fs", h), R("AK", 0, 128), H(kes[("R", h)], 1), OP.add, OP.min)
-            cp(H("kR", h), H(kes[("R", h)], 1))
-        run_units([("I", "vI", "TI", None, 0)])
+        run_units([i0])
         scans("vI", 1, ("mxB", "mnB"), True)
+        key(i0)
         act(R("SIs"), R("SIT", 0, 256))
-        tt(R("rm"), R("Fs", 0, 256), R("kR"), OP.is_equal, R("BL", 16, 32))
         floor2("TI", 1)
         floor2("CI", 1, 256)
-        run_units([("I", "vI", "TI", "CI", 1)])
-        pick([("I", "RSI", 0, 0), ("I", "RSI", 1, 0)])
+        run_units([i1])
+        key(i1)
+        run_units([r0])
+        weave(pick([("I", "RSI", 0, 0), ("I", "RSI", 1, 0)]))
         cp(R("pk"), R("RSI", *E16))
         ts(R("si"), R("pk"), 4095, OP.bitwise_and)
         tt(R("ex"), R("si"), R("MI"), OP.mult, BL)
         for h in range(2):
             mm(R("MS0", h * 8, h * 8 + 8), H("ex", h), R("CC"))
         cp(R("sU"), R("MS0", 0, 16))
+        run_units([r1])
         cp(R("nU"), R("NBw"), R("sU"))
         for h in range(2):
             gather("vN", "nU", h)
-        tt(R("dm"), R("OWw", 0, S), R("MIb"), OP.mult, R("sU"))
-        cp(R("bG"), R("OWw", 0, S), R("sU"))
-        scan(R("bs"), R("m0", 0, 256), R("dm"), OP.mult, OP.add)
-        cp(R("sF"), R("sU"))
-        cp(R("bU"), R("bs", *E16))
-        cp(R("CB"), R("CR"), R("bU"))
-        for h in range(2):
-            mm(H("MS0", h), H("CB", h), R("Ib"))
-        pick([("I", "RSI", 0, 1), ("I", "RSI", 1, 1)])
+
+        def opponents():
+            yield tt(R("dm"), R("OWw", 0, S), R("MIb"), OP.mult, R("sU"))
+            yield cp(R("bG"), R("OWw", 0, S), R("sU"))
+            yield scan(R("bs"), R("m0", 0, 256), R("dm"), OP.mult, OP.add)
+            yield cp(R("sF"), R("sU"))
+            yield cp(R("bU"), R("bs", *E16))
+            yield ts(R("nF"), R("nU"), R("pf", 1, 2), OP.add)
+            yield cp(R("CB"), R("CR"), R("bU"))
+            flip("CB", "MS0", "Ib")
+
+        weave(opponents(), pick([("I", "RSI", 0, 1), ("I", "RSI", 1, 1)]))
+        key(r0)
         for h in range(2):
             cp(H("TB", h), H("MS0", h))
-        ts(R("nF"), R("nU"), R("pf", 1, 2), OP.add)
         flip("nF", "SIT", "If")
-        th = "TH"
         if t == 0:
             consts_late()
-            th = "TH0"
-        else:
-            mm(R("MS0", 0, 1), R("o6"), R("wc"))
-            cp(R("wi"), R("MS0", 0, 1))
-            ts(R("wj"), R("wi"), 63, OP.bitwise_and)
-            ts(R("w16"), R("wj"), 16.0, OP.mult)
-            ts(R("TH"), R("TH0"), R("w16"), OP.add)
-
-        def judge(who, h):
-            res = "NSI" if who == "NI" else "NSR"
-            tt(H("fI" if who == "NI" else "fR", h), H(kes[(who, h)], 0), R(th), OP.is_lt)
-            pick([(who, res, h, 0), (who, res, h, 1)])
-
-        run_units([("NR", "vN", "TB", "CB", 0)])
         offs = [sum(256 - 16 * x for x in range(c)) for c in range(16)]
         for c in range(16):
             ts(R("EQ", offs[c], offs[c] + 256 - 16 * c), R("bG", 16 * c, 256), R("bs", 16 * c + 15, 16 * c + 16), OP.is_equal)
-        mm(R("MS0", 0, 256), R("W0"), R("EQ", 0, 256), True, False)
-        for c in range(16):
-            if c < 15:
-                mm(R("MS0", 16 * c + 16, 256), R("W1"), R("EQ", offs[c] + 16, offs[c] + 256 - 16 * c), False, False)
-            mm(R("MS0", 16 * c, 16 * c + 16), R("W2"), R("EQ", offs[c], offs[c] + 16), False, c == 15)
-        judge("NR", 0)
-        tt(R("fd"), R("MS0", 0, 256), R("thd"), OP.is_lt)
-        tt(R("fG"), R("MS0", 0, 256), R("thr"), OP.is_lt)
+
+        def fighters():
+            mm(R("MS0", 0, 256), R("W0"), R("EQ", 0, 256), True, False)
+            for c in range(16):
+                if c < 15:
+                    mm(R("MS0", 16 * c + 16, 256), R("W1"), R("EQ", offs[c] + 16, offs[c] + 256 - 16 * c), False, False)
+                mm(R("MS0", 16 * c, 16 * c + 16), R("W2"), R("EQ", offs[c], offs[c] + 16), False, c == 15)
+
+        def judge(who, h):
+            res = "NSI" if who == "NI" else "NSR"
+            yield tt(H("fI" if who == "NI" else "fR", h), H(kes[(who, h)], 0), R(th), OP.is_lt)
+            yield from pick([(who, res, h, 0), (who, res, h, 1)])
 
         def lists():
-            scan(R("fs"), R("m0", 0, 256), R("fd"), OP.mult, OP.add)
-            tt(R("w1"), R("sF"), R("ks", 0, 16), OP.subtract)
-            tt(R("w2"), R("bs", *E16), R("ks", 16, 32), OP.subtract)
-            tt(R("w1"), R("w1"), R("fs", *E16), OP.mult)
-            tt(R("w2"), R("w2"), R("fs", *E16), OP.mult)
-            tt(R("w1"), R("w1"), R("ks", 0, 16), OP.add)
-            tt(R("w2"), R("w2"), R("ks", 16, 32), OP.add)
-            cp(R("sWU"), R("w1"))
-            cp(R("bWU"), R("w2"))
-            fill(R("ZRw", 0, 256), 0.0)
-            tt(R("d3"), R("RSI", *E16b), R("RSI", *E16), OP.subtract)
+            yield tt(R("fd"), R("MS0", 0, 256), R("thd"), OP.is_lt)
+            yield tt(R("fG"), R("MS0", 0, 256), R("thr"), OP.is_lt)
+            yield scan(R("fs"), R("m0", 0, 256), R("fd"), OP.mult, OP.add)
+            yield tt(R("w1"), R("sF"), R("ks", 0, 16), OP.subtract)
+            yield tt(R("w2"), R("bs", *E16), R("ks", 16, 32), OP.subtract)
+            yield tt(R("w1"), R("w1"), R("fs", *E16), OP.mult)
+            yield tt(R("w2"), R("w2"), R("fs", *E16), OP.mult)
+            yield tt(R("w1"), R("w1"), R("ks", 0, 16), OP.add)
+            yield tt(R("w2"), R("w2"), R("ks", 16, 32), OP.add)
+            yield cp(R("sWU"), R("w1"))
+            yield cp(R("bWU"), R("w2"))
+            yield fill(R("ZRw", 0, 256), 0.0)
+            yield tt(R("d3"), R("RSI", *E16b), R("RSI", *E16), OP.subtract)
             if not last:
-                cp(R("vS"), R("Xw", 0, S), R("sU"))
-                ts(R("vT"), R("vS"), -8.0, OP.add, 0.0, OP.max)
+                yield cp(R("vS"), R("Xw", 0, S), R("sU"))
+                yield ts(R("vT"), R("vS"), -8.0, OP.add, 0.0, OP.max)
 
-        ni0, ni1 = ("NI", "vN", "TI", None, 0), ("NI", "vN", "TI", None, 1)
-        run_units([ni0, ni1, ("NR", "vN", "TB", None, 1)], {ni0: lists, ni1: lambda: judge("NI", 0)})
-        judge("NI", 1)
-        judge("NR", 1)
+        run_units([nr0], {0: fighters})
+        key(r1)
+        for h in range(2):
+            scan(H("FR", h), R("AK", 0, 128), H(kes[("R", h)], 1), OP.add, OP.min)
+            cp(H("kR", h), H(kes[("R", h)], 1))
+        key(nr0)
+        tt(R("rm"), R("FR"), R("kR"), OP.is_equal, R("BL", 16, 32))
+
+        def first():
+            weave(judge("NR", 0))
+            weave(lists())
+
+        def second():
+            key(ni1)
+            weave(judge("NI", 0))
+
+        run_units([ni0, ni1, nr1], {0: first, ni0: lambda: key(ni0), ni1: second})
+        key(nr1)
+        weave(judge("NI", 1))
+        weave(judge("NR", 1))
         flip("rm", "SIT", "Ib")
         scan(R("PC", 16, 272), R("fI"), R("fR"), OP.add, OP.subtract)
         tt(R("d1"), R("NSI", *E16), R("NSR", *E16b), OP.subtract)
@@ -482,30 +501,31 @@ def rank_program(g, core, T, topo):
         tt(R("Tm"), R("Mi"), R("SIT", 256, 512), OP.max)
         ts(R("Tm2"), R("Tm"), 4095, OP.bitwise_and)
         cp(R("SIT", 0, 256), R("Tm2"))
-
-        def owners():
-            ts(R("BC1", 0, 256), R("zG"), 262144.0, OP.is_ge)
-            tt(R("ov"), R("bG"), R("BC1", 0, 256), OP.add)
-            ts(R("BC1", 256, 512), R("ov"), 256.0, OP.is_ge, -256.0, OP.mult)
-            tt(R("ow"), R("ov"), R("BC1", 256, 512), OP.add)
-            scat(R("OWw"), R("sWU"), R("ow"))
-
+        ts(R("BC1", 0, 256), R("zG"), 262144.0, OP.is_ge)
+        tt(R("ov"), R("bG"), R("BC1", 0, 256), OP.add)
+        ts(R("BC1", 256, 512), R("ov"), 256.0, OP.is_ge, -256.0, OP.mult)
+        tt(R("ow"), R("ov"), R("BC1", 256, 512), OP.add)
         if last:
-            owners()
+            scat(R("OWw"), R("sWU"), R("ow"))
             waits("G", need("G", [R("OWw", 0, S)], []))
             g.dma_start(T.yown[:, :], T.c_OWw[0::16, 0:S]).then_inc(T.sem.dyo, 16)
             total["dyo"] = 16
         tt(R("Tm"), R("Din%d" % t), R("SIT", 0, 256), OP.max)
         ts(R("Mi"), R("Tm"), 4095, OP.bitwise_and)
-        if not last:
-            cp(R("Mu%d" % (t + 1)), R("Mi"))
-            send(R("Mu%d" % (t + 1)), "Lin%d" % (t + 1), T.cores[(rank + 2 + t) % N], "aL%d" % (t + 1), "lL%d" % (t + 1))
-            owners()
-            tt(R("wf"), R("BC1", 0, 256), R("fG"), OP.mult)
-            rsum(R("wc"), R("wf"))
-        else:
+        if last:
             cp(R("Mo"), R("Mi"))
             dma("dy", [(T.ym[:, :], T.c_Mo[:, :])], [R("Mo")], [])
+        else:
+            cp(R("Mu%d" % (t + 1)), R("Mi"))
+            send(R("Mu%d" % (t + 1)), "Lin%d" % (t + 1), T.cores[(rank + 2 + t) % N], "aL%d" % (t + 1), "lL%d" % (t + 1))
+            scat(R("OWw"), R("sWU"), R("ow"))
+            tt(R("wf"), R("BC1", 0, 256), R("fG"), OP.mult)
+            rsum(R("wc"), R("wf"))
+            mm(R("MS0", 0, 1), R("o6"), R("wc"))
+            cp(R("wi"), R("MS0", 0, 1))
+            ts(R("wj"), R("wi"), 63, OP.bitwise_and)
+            ts(R("w16"), R("wj"), 16.0, OP.mult)
+            ts(R("TH"), R("TH0"), R("w16"), OP.add)
     for s in sorted(total):
         if known["G"].get(s, 0) < total[s]:
             g.wait_ge(T.sem[s], total[s])

from concourse.mybir import dt, AluOpType, AxisListType, ActivationFunctionType

S, L, RO = 2176, 256, 3
OP = AluOpType
AF = ActivationFunctionType

SCRATCH = {}
ALIAS = {}


def _d(name, where, shape, dtype):
    SCRATCH[name] = (where, shape, dtype)


for _t, _l in (
        ("bfloat16", "Xw:2560 OWw:2560 ob:136 vR:4096 vI:4096 vN:4096 mxA:2048 mnA:2048 mxB:2048 mnB:2048 CR:256 CI:256 CB:256 "
                     "TR:256 TI:256 TB:256 mA:2048 mB:2048 mC:2048 mD:2048 rm:256 bG:256 dm:256 bs:256 EQ:4096 fG:256 fd:256 "
                     "fs:256 vS:256 vT:256 fI:256 fR:256 mh:128 Nb:128 BA:16 E:2048 one:256 hf:2048 m0:1024 a0:1024 BK:256 "
                     "BK1:256 BC:256 BM:16 BV:16 KR:256 Ib:128 W1:128 W2:128 W0:128 MIb:256"),
        ("float32", "ZRw:640 Mo:256 kR:256 FR:256 thd:256 Fs:512 nw:512 np:512 RSI:512 NSI:512 NSR:512 MF:256 SIs:256 ex:256 nF:256 "
                    "PC:272 mk2:256 DL:256 ez:256 zG:256 ov:256 ow:256 wf:256 TH:128 TH0:128 sF32:256 pf:8 AK:256 mkf:256 "
                    "If:128 thr:256 pw:256 pv:256 CC:8 MI:256 ii:256 ks:32 o6:128 B8:128"),
        ("int32", "NBw:2176 Mi:256 Tm:256 Tm2:256 oi:136 sI32:64 pi:4 bi:32 thi:1"),
        ("uint16", "nU:256 sU16:64 BL:32")):
    for _x in _l.split():
        _d("c_" + _x.split(":")[0], "sbuf", [128, int(_x.split(":")[1])], _t)
for _k, _n in enumerate(("sF", "w1", "w2", "dc", "won", "d1", "d2", "d3", "zi", "zr", "ch")):
    ALIAS[_n] = ("c_sF32", 16 * _k, 16)
for _k, _n in enumerate(("wc", "w16", "thf")):
    ALIAS[_n] = ("c_sF32", 192 + 16 * _k, 1)
for _k, (_n, _c) in enumerate((("pk", 16), ("si", 16), ("wi", 1), ("wj", 1))):
    ALIAS[_n] = ("c_sI32", 16 * _k, _c)
for _k, _n in enumerate(("sU", "bU", "sWU", "bWU")):
    ALIAS[_n] = ("c_sU16", 16 * _k, 16)
for _t in range(RO):
    _d("Mu%d" % _t, "sbuf", [128, 256], "uint16")
    _d("Lin%d" % _t, "sbuf", [128, 256], "uint16")
    _d("Do%d" % _t, "sbuf", [128, 256], "float32")
    _d("Din%d" % _t, "sbuf", [128, 256], "float32")
for _n in ("BC0", "BC1", "BC2", "BC3", "KE0", "KE1", "SIT", "MS0"):
    _d("p_" + _n, "psum", [128, 512], "float32")
_d("ownd", "dram", [8, S], "bfloat16")

SEMAPHORES = (["qV", "qS", "qP", "qG", "dx", "dm", "dn", "do", "dod", "dor", "dth", "dy", "dyo"]
              + [n + "%d" % t for n in ("aL", "aD", "lL", "lD") for t in range(RO)])


def rank_program(g, core, T, topo):
    rank = T.rank_of(core)
    if rank is None:
        return
    N = len(T.cores)
    Q = {"V": g.vector, "S": g.scalar, "P": g.tensor, "G": g, "Y": g.sync}
    cnt = {"V": 0, "S": 0, "P": 0, "G": 0}
    known = {q: {} for q in Q}
    snap = {}
    acc = {}
    total = {}

    def R(name, c0=0, c1=None, st=1, p0=0, p1=128):
        o = 0
        if name in ALIAS:
            name, o, w = ALIAS[name]
        else:
            if not (name in SCRATCH):
                name = "c_" + name if "c_" + name in SCRATCH else "p_" + name
            w = SCRATCH[name][1][1]
        c1 = o + (w if c1 is None else c1)
        c0 = o + c0
        ap = T[name][p0:p1, c0:c1] if st == 1 else T[name][p0:p1, c0:c1:st]
        return (ap, name, c0, c1)

    def H(name, h, o=0):
        return R(name, o + h * 128, o + h * 128 + 128)

    def ind(win, off):
        return win[0].indirect(off[0])

    def need(queue, reads, writes):
        out = {}
        for regs, wr in ((reads, False), (writes, True)):
            for r in regs:
                ps = r[1].startswith("p_")
                for (c0, c1, q, src, n, w) in acc.get(r[1], []):
                    if ps:
                        if q == queue == "P":
                            continue
                        if q == queue and (not w or wr or c0 >= r[3] or r[2] >= c1):
                            continue
                    else:
                        if c0 >= r[3] or r[2] >= c1 or not (w or wr):
                            continue
                        if q == queue and q in cnt and not w:
                            continue
                    out[src] = max(out.get(src, 0), n)
        return out

    def learn(queue, src, n):
        k = known[queue]
        k[src] = max(k.get(src, 0), n)
        for s2, n2 in snap.get((src, n), {}).items():
            k[s2] = max(k.get(s2, 0), n2)

    def waits(queue, nd):
        for src in sorted(nd, key=lambda s: -nd[s]):
            if known[queue].get(src, 0) < nd[src]:
                Q[queue].wait_ge(T.sem[src], nd[src])
                learn(queue, src, nd[src])

    def note(queue, label, src, n, reads, writes):
        snap[(src, n)] = dict(known[queue])
        for regs, wr in ((reads, False), (writes, True)):
            for r in regs:
                lst = acc.get(r[1], [])
                if wr:
                    lst = [e for e in lst if not (e[0] >= r[2] and e[1] <= r[3])]
                acc[r[1]] = lst + [(r[2], r[3], label, src, n, wr)]

    def op(queue, fn, reads, writes):
        waits(queue, need(queue, reads, writes))
        inst = fn()
        cnt[queue] += 1
        inst.then_inc(T.sem["q" + queue], 1)
        total["q" + queue] = cnt[queue]
        note(queue, queue, "q" + queue, cnt[queue], reads, writes)

    def act(out, in_, off=None, func=AF.Copy):
        src = in_[0] if off is None else ind(in_, off)
        op("S", lambda: g.scalar.activation(out[0], src, func), [in_] + ([off] if off else []), [out])

    def cp(out, in_, off=None):
        src = in_[0] if off is None else ind(in_, off)
        op("V", lambda: g.vector.tensor_copy(out[0], src), [in_] + ([off] if off else []), [out])

    def scat(win, off, in_):
        op("V", lambda: g.vector.tensor_copy(ind(win, off), in_[0]), [in_, off], [win])

    def tt(out, a, b, o, off=None):
        src = a[0] if off is None else ind(a, off)
        op("V", lambda: g.vector.tensor_tensor(out[0], src, b[0], o), [a, b] + ([off] if off else []), [out])

    def ts(out, a, s1, o1, s2=None, o2=None):
        rd = [a]
        x1 = s1
        if isinstance(s1, tuple):
            rd.append(s1)
            x1 = s1[0]
        if o2 is None:
            op("V", lambda: g.vector.tensor_scalar(out[0], a[0], x1, None, o1), rd, [out])
        else:
            op("V", lambda: g.vector.tensor_scalar(out[0], a[0], x1, s2, o1, o2), rd, [out])

    def scan(out, a, b, o1, o2):
        op("V", lambda: g.vector.tensor_tensor_scan(out[0], a[0], b[0], 0.0, o1, o2), [a, b], [out])

    def fill(out, x):
        op("V", lambda: g.vector.memset(out[0], x), [], [out])

    def mm(out, l, r, start=True, stop=True):
        op("P", lambda: g.tensor.matmul(out[0], l[0], r[0], start, stop), [l, r], [out])

    def rsum(out, in_):
        op("V", lambda: g.vector.tensor_reduce(out[0], in_[0], AxisListType.X, OP.add), [in_], [out])

    def iota(out, pat, base, mult):
        op("G", lambda: g.iota(out[0], pat, base, mult, allow_small_or_imprecise_dtypes=True), [], [out])

    def asel(out, in_, pat, cmp_, base, mult):
        op("G", lambda: g.affine_select(out[0], in_[0], pat, cmp_, 0.0, base, mult), [in_], [out])

    def dma(sem, pairs, reads, writes, queue="Y"):
        waits(queue, need(queue, reads, writes))
        for o, i in pairs:
            Q[queue].dma_start(o, i).then_inc(T.sem[sem], 16)
        total[sem] = 16 * len(pairs)
        note(queue, "D", sem, total[sem], reads, writes)

    def send(buf, land, dst, asem, lsem):
        eng = topo.engines(core, dst)[:8]
        m = 0
        for e in eng:
            m |= 1 << e
        waits("G", need("G", [buf], []))
        rid, pid = topo.addr(dst, core)
        g.remote_dma(T[land][:], buf[0], T.sem[asem], T.sem[lsem], pid, rid, m)
        total[lsem] = len(eng)

    def arrive(land, asem, src):
        n = len(topo.engines(src, core)[:8])
        total[asem] = n
        acc[land] = [(0, 256, "X", asem, n, True)]

    def weave(*gens):
        gens = list(gens)
        while gens:
            for x in list(gens):
                if next(x, 0) == 0:
                    gens.remove(x)

    dma("dm", [(T.c_Mi[:, :], T.m0[:, :])], [], [R("Mi")], "S")
    dma("dx", [(T.c_Xw[:, 0:S], T.x0[:, :])], [], [R("Xw", 0, S)])
    dma("do", [(T.c_oi[:, :], T.own0[:, :])], [], [R("oi")])
    dma("dth", [(T.c_thi[0:8, :], T.th[:, :])], [], [R("thi", 0, 1)])
    dma("dn", [(T.c_NBw[:, :], T.nb[:, :])], [], [R("NBw")])
    fill(R("one"), 1.0)
    fill(R("m0"), 1.0)
    fill(R("a0"), 0.0)
    fill(R("hf"), 0.5)
    fill(R("m0", 0, 1024, 16), 0.0)
    fill(R("a0", 0, 1024, 16), 512.0)
    cp(R("Mu0"), R("Mi"))
    for t in range(RO):
        arrive("Lin%d" % t, "aL%d" % t, T.cores[(rank - 1 - t) % N])
        arrive("Din%d" % t, "aD%d" % t, T.cores[(rank + 1 + t) % N])
    iota(R("pi", 0, 1), [[0, 1]], 0, 1)
    iota(R("bi", 0, 16), [[1, 16]], 0, 0)
    iota(R("bi", 16, 32), [[16, 16]], 15, 0)
    asel(R("Ib"), R("one", 0, 128), [[-1, 128]], OP.is_equal, 0, 1)
    send(R("Mu0"), "Lin0", T.cores[(rank + 1) % N], "aL0", "lL0")
    asel(R("E"), R("hf"), [[-1, 128], [0, 16]], OP.is_equal, 0, 1)
    asel(R("BK1"), R("one", 0, 256), [[0, 2], [-16, 8], [0, 16]], OP.is_ge, 0, 1)
    asel(R("BK"), R("BK1"), [[0, 2], [16, 8], [0, 16]], OP.is_ge, 15, -1)
    iota(R("KR"), [[-15, 2], [0, 8], [1, 16]], 0, 0)
    iota(R("ii"), [[0, 16], [1, 16]], 0, 0)
    iota(R("ks", 0, 16), [[16, 16]], S, 1)
    iota(R("ks", 16, 32), [[16, 16]], 256, 1)

    def consts_early():
        cp(R("ob"), R("oi"))
        dma("dod", [(T.ownd[:, :], T.c_ob[:, :])], [R("ob")], [("", "ownd", 0, S)])
        dma("dor", [(T.c_OWw[i::16, 0:S], T.ownd[:, :]) for i in range(16)], [("", "ownd", 0, S)], [R("OWw", 0, S)])
        ts(R("pi", 1, 2), R("pi", 0, 1), 15, OP.bitwise_and)
        cp(R("If"), R("Ib"))
        cp(R("pf", 0, 1), R("pi", 1, 2))
        ts(R("Nb"), R("Ib"), -1.0, OP.mult)
        ts(R("pf", 1, 2), R("pf", 0, 1), 1.0, OP.add, 4096.0, OP.mult)
        fill(R("mh"), -0.5)
        cp(R("BL"), R("bi"))

    def consts_mid():
        ts(R("BM", 0, 8), R("BK", 0, 128, 16), 32.0, OP.mult)
        ts(R("BM", 8, 16), R("BK", 0, 128, 16), -32.0, OP.mult)
        ts(R("BV", 0, 8), R("BK", 0, 128, 16), -16.0, OP.mult)
        ts(R("BV", 8, 16), R("BK", 0, 128, 16), 16.0, OP.mult)
        ts(R("BC", 0, 128), R("BK", 0, 128), -8.0, OP.mult)
        ts(R("BC", 128, 256), R("BK", 0, 128), 8.0, OP.mult)
        ts(R("BA"), R("BV"), -1.0, OP.mult)
        fill(R("AK"), 0.0)
        fill(R("mkf"), 1.0)
        ts(R("MI"), R("ii"), R("pf", 0, 1), OP.is_equal)
        fill(R("AK", 0, 256, 16), 1000000.0)
        fill(R("mkf", 0, 256, 16), 0.0)
        cp(R("MIb"), R("MI"))
        cp(R("CC"), R("BK", 0, 128, 16))

    def consts_late():
        fill(R("pw"), 0.0)
        ts(R("pv"), R("mkf"), 0.5, OP.mult)
        fill(R("pw", 0, 256, 16), 2.0)
        scan(R("thr"), R("pv"), R("pw"), OP.mult, OP.add)
        fill(R("W0"), 0.0)
        tt(R("thd"), R("thr"), R("MI"), OP.mult)
        fill(R("o6"), 0.0625)
        rsum(R("pf", 2, 3), R("thd", 0, 16))
        ts(R("W1"), R("BK", 0, 128), 64.0, OP.mult)
        ts(R("W2"), R("BK", 0, 128), R("pf", 2, 3), OP.mult, 0.5, OP.mult)
        fill(R("PC", 0, 16), 0.0)
        cp(R("thf", 0, 1, 1, 0, 8), R("thi", 0, 1, 1, 0, 8))
        ts(R("B8", 0, 128, 1, 0, 8), R("E", 0, 128, 1, 0, 8), R("thf", 0, 1, 1, 0, 8), OP.mult, 512.0, OP.mult)
        mm(R("MS0", 0, 128), R("o6", 0, 128, 1, 0, 8), R("B8", 0, 128, 1, 0, 8))
        cp(R("TH0"), R("MS0", 0, 128))

    def gather(v, lst, h):
        for c in range(2):
            a = h * 128 + c * 64
            act(R(v, a * 16, a * 16 + 1024), R("Xw", 0, S), R(lst, a, a + 64))

    def scans(v, h, bufs, nat):
        mx, mn = bufs
        for c in range(2):
            x = R(v, h * 2048 + c * 1024, h * 2048 + c * 1024 + 1024)
            scan(R(mx, c * 1024, c * 1024 + 1024), R("m0"), x, OP.mult, OP.max)
            scan(R(mn, c * 1024, c * 1024 + 1024), R("a0"), x, OP.add, OP.min)
        a, b = R(mx, 15, 2048, 16), R(mn, 15, 2048, 16)
        one, mh = R("one", 0, 128, 1, 0, 1), R("mh", 0, 128, 1, 0, 1)
        mm(H("MS0", h), a, R("Ib"), True, False)
        mm(H("MS0", h), b, R("Ib"), False, False)
        mm(H("MS0", h), one, mh, False, True)
        if nat:
            mm(H("MS0", h, 256), R("Ib"), a, True, False)
            mm(H("MS0", h, 256), R("Ib"), b, False, False)
            mm(H("MS0", h, 256), one, mh, False, True)

    def floor2(out, h, o=0):
        ts(H(out, h), H("MS0", h, o), 16777216.0, OP.add, 16777216.0, OP.subtract)

    bcn, ken, mbn, bank, kes, mbs = [0], [0], [0], {}, {}, {}

    def bc(u, b):
        k = "BC%d" % (bcn[0] % 4)
        bcn[0] += 1
        bank[(u, b)] = k
        mm(R(k), H(u[2], u[4]), R("E", b * 512, b * 512 + 512), True, u[3] is not None)
        if u[3] is None:
            mm(R(k), R("Nb"), R(u[1], u[4] * 2048 + b * 512, u[4] * 2048 + b * 512 + 512), False, True)

    def key(u):
        ke = "KE%d" % (ken[0] % 2)
        ken[0] += 1
        h, mb = u[4], mbs[u]
        mm(R(ke, 0, 256), R("one", 0, 128, 1, 0, 1), R("KR", 0, 256, 1, 0, 1), True, False)
        if u[3] is not None:
            mm(R(ke, 0, 256), H(u[3], h), R("BC"), False, False)
            for k in range(16):
                mm(R(ke, k, 256, 16), R(u[1], h * 2048 + k, h * 2048 + 2048, 16), R("BV"), False, False)
        for k in range(16):
            mm(R(ke, k, 256, 16), R(mb, k, 2048, 16), R("BM" if u[3] is not None else "BA"), False, k == 15)
        kes[(u[0], h)] = ke

    def run_units(units, hooks={}):
        flat = [(u, b) for u in units for b in range(4)]
        for u, b in flat[:4]:
            bc(u, b)
        if 0 in hooks:
            hooks[0]()
        for n, (u, b) in enumerate(flat):
            if b == 0:
                mbs[u] = "m" + "ABCD"[mbn[0] % 4]
                mbn[0] += 1
            o = R(mbs[u], b * 512, b * 512 + 512)
            if u[3] is None:
                act(o, R(bank[(u, b)]), None, AF.Abs)
            else:
                tt(o, R(u[1], u[4] * 2048 + b * 512, u[4] * 2048 + b * 512 + 512), R(bank[(u, b)]), OP.max)
            if n + 4 < len(flat):
                bc(*flat[n + 4])
            if b == 3 and u in hooks:
                hooks[u]()

    def pick(jobs):
        jobs = [(H(kes[(who, h)], x), H(res, 2 * x + h), h, n) for n, (who, res, h, x) in enumerate(jobs)]
        for k, res, h, n in jobs:
            yield scan(H("Fs", n), R("AK", 0, 128), k, OP.add, OP.min)
        for k, res, h, n in jobs:
            yield tt(H("nw", n), k, H("Fs", n), OP.is_equal)
        for k, res, h, n in jobs:
            yield tt(H("np", n), H("nw", n), H("SIT", h), OP.mult)
        for k, res, h, n in jobs:
            yield scan(res, R("mkf", 0, 128), H("np", n), OP.mult, OP.max)

    def flip(src, ps, idn):
        for h in range(2):
            mm(H(ps, h), H(src, h), R(idn))

    E16 = (15, 256, 16)
    E16b = (271, 512, 16)
    BL = R("BL", 0, 16)
    for t in range(RO):
        last = t == RO - 1
        mu, li, do = "Mu%d" % t, "Lin%d" % t, "Do%d" % t
        r0, r1 = ("R", "vR", "TR", None, 0), ("R", "vR", "TR", None, 1)
        i0, i1 = ("I", "vI", "TI", None, 0), ("I", "vI", "TI", "CI", 1)
        ni0, ni1 = ("NI", "vN", "TI", None, 0), ("NI", "vN", "TI", None, 1)
        nr0, nr1 = ("NR", "vN", "TB", "CB", 0), ("NR", "vN", "TB", None, 1)
        th = "TH" if t else "TH0"
        gather("vR", mu, 0)
        gather("vR", mu, 1)
        if t == 0:
            consts_early()
        scans("vR", 0, ("mxA", "mnA"), True)
        if t == 0:
            consts_mid()
        scans("vR", 1, ("mxB", "mnB"), True)
        floor2("TR", 0)
        floor2("CR", 0, 256)
        gather("vI", li, 0)
        gather("vI", li, 1)
        floor2("TR", 1)
        floor2("CR", 1, 256)
        ts(R("MF"), R(li), R("pf", 1, 2), OP.add)
        flip("MF", "SIT", "If")
        scans("vI", 0, ("mxA", "mnA"), False)
        floor2("TI", 0)
        run_units([i0])
        scans("vI", 1, ("mxB", "mnB"), True)
        key(i0)
        act(R("SIs"), R("SIT", 0, 256))
        floor2("TI", 1)
        floor2("CI", 1, 256)
        run_units([i1])
        key(i1)
        run_units([r0])
        weave(pick([("I", "RSI", 0, 0), ("I", "RSI", 1, 0)]))
        cp(R("pk"), R("RSI", *E16))
        ts(R("si"), R("pk"), 4095, OP.bitwise_and)
        tt(R("ex"), R("si"), R("MI"), OP.mult, BL)
        for h in range(2):
            mm(R("MS0", h * 8, h * 8 + 8), H("ex", h), R("CC"))
        cp(R("sU"), R("MS0", 0, 16))
        run_units([r1])
        cp(R("nU"), R("NBw"), R("sU"))
        for h in range(2):
            gather("vN", "nU", h)

        def opponents():
            yield tt(R("dm"), R("OWw", 0, S), R("MIb"), OP.mult, R("sU"))
            yield cp(R("bG"), R("OWw", 0, S), R("sU"))
            yield scan(R("bs"), R("m0", 0, 256), R("dm"), OP.mult, OP.add)
            yield cp(R("sF"), R("sU"))
            yield cp(R("bU"), R("bs", *E16))
            yield ts(R("nF"), R("nU"), R("pf", 1, 2), OP.add)
            yield cp(R("CB"), R("CR"), R("bU"))
            flip("CB", "MS0", "Ib")

        weave(opponents(), pick([("I", "RSI", 0, 1), ("I", "RSI", 1, 1)]))
        key(r0)
        for h in range(2):
            cp(H("TB", h), H("MS0", h))
        flip("nF", "SIT", "If")
        if t == 0:
            consts_late()
        offs = [sum(256 - 16 * x for x in range(c)) for c in range(16)]
        for c in range(16):
            ts(R("EQ", offs[c], offs[c] + 256 - 16 * c), R("bG", 16 * c, 256), R("bs", 16 * c + 15, 16 * c + 16), OP.is_equal)

        def fighters():
            mm(R("MS0", 0, 256), R("W0"), R("EQ", 0, 256), True, False)
            for c in range(16):
                if c < 15:
                    mm(R("MS0", 16 * c + 16, 256), R("W1"), R("EQ", offs[c] + 16, offs[c] + 256 - 16 * c), False, False)
                mm(R("MS0", 16 * c, 16 * c + 16), R("W2"), R("EQ", offs[c], offs[c] + 16), False, c == 15)

        def judge(who, h):
            res = "NSI" if who == "NI" else "NSR"
            yield tt(H("fI" if who == "NI" else "fR", h), H(kes[(who, h)], 0), R(th), OP.is_lt)
            yield from pick([(who, res, h, 0), (who, res, h, 1)])

        def lists():
            yield tt(R("fd"), R("MS0", 0, 256), R("thd"), OP.is_lt)
            yield tt(R("fG"), R("MS0", 0, 256), R("thr"), OP.is_lt)
            yield scan(R("fs"), R("m0", 0, 256), R("fd"), OP.mult, OP.add)
            yield tt(R("w1"), R("sF"), R("ks", 0, 16), OP.subtract)
            yield tt(R("w2"), R("bs", *E16), R("ks", 16, 32), OP.subtract)
            yield tt(R("w1"), R("w1"), R("fs", *E16), OP.mult)
            yield tt(R("w2"), R("w2"), R("fs", *E16), OP.mult)
            yield tt(R("w1"), R("w1"), R("ks", 0, 16), OP.add)
            yield tt(R("w2"), R("w2"), R("ks", 16, 32), OP.add)
            yield cp(R("sWU"), R("w1"))
            yield cp(R("bWU"), R("w2"))
            yield fill(R("ZRw", 0, 256), 0.0)
            yield tt(R("d3"), R("RSI", *E16b), R("RSI", *E16), OP.subtract)
            if not last:
                yield cp(R("vS"), R("Xw", 0, S), R("sU"))
                yield ts(R("vT"), R("vS"), -8.0, OP.add, 0.0, OP.max)

        run_units([nr0], {0: fighters})
        key(r1)
        for h in range(2):
            scan(H("FR", h), R("AK", 0, 128), H(kes[("R", h)], 1), OP.add, OP.min)
            cp(H("kR", h), H(kes[("R", h)], 1))
        key(nr0)
        tt(R("rm"), R("FR"), R("kR"), OP.is_equal, R("BL", 16, 32))

        def first():
            weave(judge("NR", 0))
            weave(lists())

        def second():
            key(ni1)
            weave(judge("NI", 0))

        run_units([ni0, ni1, nr1], {0: first, ni0: lambda: key(ni0), ni1: second})
        key(nr1)
        weave(judge("NI", 1))
        weave(judge("NR", 1))
        flip("rm", "SIT", "Ib")
        scan(R("PC", 16, 272), R("fI"), R("fR"), OP.add, OP.subtract)
        tt(R("d1"), R("NSI", *E16), R("NSR", *E16b), OP.subtract)
        tt(R("dc"), R("PC", 31, 272, 16), R("PC", *E16), OP.subtract)
        tt(R("d2"), R("NSI", *E16b), R("NSR", *E16), OP.subtract)
        ts(R("won"), R("dc"), 0.0, OP.is_gt)
        ts(R("d2"), R("d2"), 262144.0, OP.add)
        tt(R("d3"), R("d3"), R("won"), OP.mult)
        tt(R("d1"), R("d1"), R("won"), OP.mult)
        tt(R("ch"), R("d3"), R("RSI", *E16), OP.add)
        tt(R("zi"), R("d1"), R("NSR", *E16b), OP.add)
        tt(R("mk2"), R("ch"), R("SIs"), OP.is_equal, BL)
        tt(R("DL"), R("zi"), R("mk2"), OP.mult, BL)
        flip("DL", "MS0", "If")
        tt(R("d2"), R("d2"), R("won"), OP.mult)
        tt(R("zr"), R("d2"), R("NSR", *E16), OP.add)
        act(R("ez"), R("zr"), BL)
        flip("ez", "BC0", "If")
        tt(R(do), R("MS0", 0, 256), R("fG"), OP.mult)
        send(R(do), "Din%d" % t, T.cores[(rank - 1 - t) % N], "aD%d" % t, "lD%d" % t)
        act(R("zG"), R("BC0", 0, 256))
        if not last:
            scat(R("Xw"), R("sWU"), R("vT"))
        scat(R("ZRw"), R("bWU"), R("zG"))
        tt(R("SIT", 256, 512), R("ZRw", 0, 256), R("SIT", 0, 256), OP.mult)
        tt(R("Tm"), R("Mi"), R("SIT", 256, 512), OP.max)
        ts(R("Tm2"), R("Tm"), 4095, OP.bitwise_and)
        cp(R("SIT", 0, 256), R("Tm2"))
        ts(R("BC1", 0, 256), R("zG"), 262144.0, OP.is_ge)
        tt(R("ov"), R("bG"), R("BC1", 0, 256), OP.add)
        ts(R("BC1", 256, 512), R("ov"), 256.0, OP.is_ge, -256.0, OP.mult)
        tt(R("ow"), R("ov"), R("BC1", 256, 512), OP.add)
        if last:
            scat(R("OWw"), R("sWU"), R("ow"))
            waits("G", need("G", [R("OWw", 0, S)], []))
            g.dma_start(T.yown[:, :], T.c_OWw[0::16, 0:S]).then_inc(T.sem.dyo, 16)
            total["dyo"] = 16
        tt(R("Tm"), R("Din%d" % t), R("SIT", 0, 256), OP.max)
        ts(R("Mi"), R("Tm"), 4095, OP.bitwise_and)
        if last:
            cp(R("Mo"), R("Mi"))
            dma("dy", [(T.ym[:, :], T.c_Mo[:, :])], [R("Mo")], [])
        else:
            cp(R("Mu%d" % (t + 1)), R("Mi"))
            send(R("Mu%d" % (t + 1)), "Lin%d" % (t + 1), T.cores[(rank + 2 + t) % N], "aL%d" % (t + 1), "lL%d" % (t + 1))
            scat(R("OWw"), R("sWU"), R("ow"))
            tt(R("wf"), R("BC1", 0, 256), R("fG"), OP.mult)
            rsum(R("wc"), R("wf"))
            mm(R("MS0", 0, 1), R("o6"), R("wc"))
            cp(R("wi"), R("MS0", 0, 1))
            ts(R("wj"), R("wi"), 63, OP.bitwise_and)
            ts(R("w16"), R("wj"), 16.0, OP.mult)
            ts(R("TH"), R("TH0"), R("w16"), OP.add)
    for s in sorted(total):
        if known["G"].get(s, 0) < total[s]:
            g.wait_ge(T.sem[s], total[s])
